import numpy as np
import ml_dtypes


def mxq(x, axis, fmt="e4m3"):
    dtype, down = {"e4m3": (ml_dtypes.float8_e4m3fn, 7), "e5m2": (ml_dtypes.float8_e5m2, 14)}[fmt]
    v = np.moveaxis(np.asarray(x, np.float32).astype(ml_dtypes.bfloat16).astype(np.float64), axis, -1)
    blocks = v.reshape(v.shape[:-1] + (-1, 32))
    amax = np.abs(blocks).max(-1, keepdims=True)
    byte = np.maximum(np.where(amax > 0, np.frexp(amax)[1] - 1 + 127, 0) - down, 1)
    scale = np.exp2(byte - 127.0)
    codes = (blocks / scale).astype(np.float32).astype(dtype).astype(np.float64)
    return np.moveaxis((codes * scale).reshape(v.shape), -1, axis)


WIDE = False


def mx_kscale(k):
    if not WIDE:
        return np.ones(k)
    levels = np.array([10, -10, 5, -5, 0])
    if k % 512:
        return np.exp2(np.random.permutation(np.resize(levels, k // 32))).repeat(32)
    a = np.empty((k // 512, 16))
    for p in range(k // 512):
        a[p, :8] = np.random.permutation(np.resize(levels, 8))
        for g in range(8):
            far = levels[np.abs(levels - a[p, g]) >= 10]
            a[p, g + 8] = far[np.random.randint(len(far))]
    return np.exp2(a.ravel()).repeat(32)


def f64(x):
    return np.asarray(x).astype(np.float64)


def striped(idx):
    return np.tile(idx.reshape(-1, 16).T, (8, 1)).astype(np.uint16)


def unstriped(offs):
    return offs[:16].T.reshape(-1).astype(np.int64)


E2M1 = np.array([0.0, 0.5, 1.0, 1.5, 2.0, 3.0, 4.0, 6.0, -0.0, -0.5, -1.0, -1.5, -2.0, -3.0, -4.0, -6.0])


def pack_weight(w, fmt):
    k, n = w.shape
    w = f64(np.asarray(w, np.float32).astype(ml_dtypes.bfloat16)).reshape(k // 32, 32, n)
    amax = np.abs(w).max(1)
    if fmt == "e4m3":
        byte = np.frexp(amax)[1] - 1 + 127 - 7
    else:
        mant, ex = np.frexp(amax / 6.0)
        byte = np.where(mant > 0.5, ex, ex - 1) + 127
    byte = np.clip(np.where(amax > 0, byte, 1), 1, 254)
    scaled = (w * np.exp2(127.0 - byte)[:, None, :]).reshape(k, n).astype(np.float32)
    by_word = np.ascontiguousarray(scaled.reshape(k // 512, 128, 4, n).transpose(0, 1, 3, 2))
    if fmt == "e4m3":
        words = by_word.astype(ml_dtypes.float8_e4m3fn).view(np.uint8)
    else:
        c = by_word.astype(ml_dtypes.float4_e2m1fn).view(np.uint8) & 0xF
        words = (c[..., 0::2] | (c[..., 1::2] << 4)).reshape(k // 512, 128, 2 * n)
    return np.ascontiguousarray(words), np.ascontiguousarray(byte.astype(np.uint8).reshape(k // 512, 16, n))


def unpack_weight(words, scales, fmt):
    g, _, n = scales.shape
    words = np.ascontiguousarray(words).reshape(g, 128, n, -1)
    if fmt == "e4m3":
        vals = words.view(ml_dtypes.float8_e4m3fn).astype(np.float64)
    else:
        nib = np.empty((g, 128, n, 4), np.uint8)
        nib[..., 0::2] = words & 0xF
        nib[..., 1::2] = words >> 4
        vals = E2M1[nib]
    vals = vals * np.repeat(np.exp2(scales.astype(np.float64) - 127.0), 8, axis=1)[..., None]
    return vals.transpose(0, 1, 3, 2).reshape(g * 512, n)


def gelu(v):
    return 0.5 * v * (1.0 + np.tanh(np.sqrt(2.0 / np.pi) * (v + 0.044715 * v**3)))


def bf(x):
    return np.asarray(x, np.float32).astype(ml_dtypes.bfloat16)


def planes(Y):
    n, m = Y.shape
    b = f64(bf(Y)).reshape(n // 32, 32, m)
    amax = np.abs(b).max(1)
    byte = np.clip(np.where(amax > 0, np.frexp(amax)[1] - 1 + 127 - 7, 1), 1, 254)
    codes = (b * np.exp2(127.0 - byte)[:, None, :]).reshape(n, m).astype(np.float32).astype(ml_dtypes.float8_e4m3fn).view(np.uint8)
    words = codes.reshape(n // 512, 128, 4, m).transpose(0, 1, 3, 2)
    return np.ascontiguousarray(words), np.ascontiguousarray(byte.astype(np.uint8).reshape(n // 512, 16, m))


K, H, N, T, S, T2, P = 1024, 1024, 384, 4096, 1024, 2048, 1024

def setup_inputs():
    n = np.random.standard_normal
    s = mx_kscale(K)[:, None]
    u = mx_kscale(H)[:, None]
    d = {}
    d["tab_words"], d["tab_scales"] = pack_weight(n((K, T)) * s, "e4m3")
    d["offs"] = striped(np.random.permutation(T)[:S])
    d["offs2"] = striped(np.random.permutation(T2)[:S])
    d["offs3"] = striped(np.random.permutation(T2)[:P])
    d["w1"] = (n((K, H)) / K**0.5 / s * u.T).astype(np.float32)
    d["w2_words"], d["w2_scales"] = pack_weight(n((K, H)) / K**0.5 / s * u.T, "e2m1")
    d["expo"] = (0.8 * np.exp(0.5 * n((H, S)))).astype(np.float32)
    d["page0"] = (n((H, T2)) * u).astype(np.float32)
    d["wgs"] = np.exp(0.3 * n((128, S))).astype(np.float32)
    d["sv"] = np.exp(0.4 * n(H)).astype(np.float32)
    d["w3"] = (0.7 * n((H, N)) / H**0.5 / u).astype(np.float32)
    d["w4_words"], d["w4_scales"] = pack_weight(n((H, N)) / H**0.5 / u, "e2m1")
    d["b4"] = (0.6 * n(N)).astype(np.float32)
    return d

def reference(tab_words, tab_scales, offs, offs2, offs3, w1, w2_words, w2_scales, expo, page0, wgs, sv, w3, w4_words, w4_scales, b4):
    v = unpack_weight(tab_words, tab_scales, "e4m3")[:, unstriped(offs)]
    base = mxq(f64(w1), 0, "e4m3").T @ v
    wind = unpack_weight(w2_words, w2_scales, "e2m1").T @ v
    h = base + f64(expo) * wind
    page = f64(page0).copy()
    page[:, unstriped(offs2)] = np.tile(f64(wgs), (H // 128, 1)) * h
    x = mxq(page[:, unstriped(offs3)] * f64(sv)[:, None], 0, "e4m3")
    lin = mxq(f64(w3), 0, "e4m3").T @ x
    bent = unpack_weight(w4_words, w4_scales, "e2m1").T @ x
    y = lin + np.tanh(bent + f64(b4)[:, None])
    words, scales = planes(page)
    return y, page, words, scales

@@ -1,0 +1,385 @@
+from contextlib import ExitStack
+
+import concourse.mybir as mybir
+
+K, H, N, T, S, T2, M = 1024, 1024, 384, 4096, 1024, 2048, 1024
+FLOPS = 2 * 2 * K * H * S + 2 * 2 * H * N * M
+
+F32 = mybir.dt.float32
+BF16 = mybir.dt.bfloat16
+I32 = mybir.dt.int32
+U32 = mybir.dt.uint32
+U16 = mybir.dt.uint16
+U8 = mybir.dt.uint8
+FP8X4 = mybir.dt.float8_e4m3fn_x4
+FP4X4 = mybir.dt.float4_e2m1fn_x4
+MULT = mybir.AluOpType.mult
+ADD = mybir.AluOpType.add
+COPY = mybir.ActivationFunctionType.Copy
+TANH = mybir.ActivationFunctionType.Tanh
+
+P = 128
+PACK = 4
+PASS = P * PACK
+BANK = 512
+TILES = H // P
+PATH = "HGGGGGGG"
+
+
+def tile_list_snow_cell_page_kernel(
+    tc, tab_words, tab_scales, offs, offs2, offs3, w1, w2_words, w2_scales, expo, page0, wgs, sv,
+    w3, w4_words, w4_scales, b4, out_0, out_1, out_2, out_3,
+):
+    nc = tc.nc
+    with ExitStack() as ctx:
+        lists = ctx.enter_context(tc.tile_pool(name="lists", bufs=1))
+        keep = ctx.enter_context(tc.tile_pool(name="keep", bufs=1))
+        ring = ctx.enter_context(tc.tile_pool(name="ring", bufs=2))
+        psum = ctx.enter_context(tc.psum_pool(name="psum", bufs=8))
+
+        def rows_of(mat, i):
+            b, t = divmod(i, PACK)
+            return mat[b * PASS : (b + 1) * PASS, :].rearrange("(p t) c -> p t c", t=PACK)[:, t, :]
+
+        def half(h):
+            return slice(h * BANK, (h + 1) * BANK)
+
+        def list_half(lst, h):
+            return lst[:, h * (BANK // 16) : (h + 1) * (BANK // 16)]
+
+        pick = lists.tile([P, S // 16], U16, name="pick")
+        put = lists.tile([P, S // 16], U16, name="put")
+        read = lists.tile([P, M // 16], U16, name="read")
+        nc.sync.dma_start(pick[:], offs)
+        nc.sync.dma_start(put[:], offs2)
+        nc.sync.dma_start(read[:], offs3)
+
+        def load_scale_rows(tile, src):
+            nc.vector.memset(tile[:].bitcast(I32), 0)
+            for q in range(4):
+                nc.gpsimd.dma_start(
+                    out=tile[32 * q : 32 * q + 4, :, :].bitcast(I32),
+                    in_=src[:, 4 * q : 4 * q + 4, :].rearrange("a r c -> r a c").bitcast(I32),
+                )
+
+        tab_sc = keep.tile([P, 2, T], U8, name="tab_sc", tag="tabsc_xplanes", align_bytes=64)
+        w2_sc_raw = keep.tile([P, 2, H], U8, name="w2_sc_raw", tag="w1_first", align_bytes=64)
+        w4_sc = keep.tile([P, 2, N], U8, name="w4_sc", align_bytes=64)
+        load_scale_rows(tab_sc, tab_scales)
+        load_scale_rows(w2_sc_raw, w2_scales)
+        load_scale_rows(w4_sc, w4_scales)
+
+        w2_raw = ring.tile([P, 2, 2 * H], U8, name="w2_raw", tag="xg", align_bytes=64)
+        nc.sync.dma_start(out=w2_raw[:].bitcast(I32), in_=w2_words.rearrange("a p c -> p a c").bitcast(I32))
+
+        w1_codes = {}
+        w1_sc = keep.tile([P, 2, 2 * PASS], U8, name="w1_sc", align_bytes=64)
+
+        def load_w1(b):
+            raws = []
+            for a in range(2):
+                raw = ring.tile([P, PACK, PASS], F32, name="w1_raw", tag="raw_inter", align_bytes=64)
+                src = w1[a * PASS : (a + 1) * PASS, b * PASS : (b + 1) * PASS]
+                nc.sync.dma_start(out=raw[:], in_=src.rearrange("(p j) c -> p j c", j=PACK))
+                raws.append(raw)
+            return raws
+
+        def quantise_w1(b, raws):
+            grouped = keep.tile([P, 2 * PASS * PACK], BF16, name="w1_grouped", tag=("grouped_v", "grouped")[b], align_bytes=64)
+            for a in range(2):
+                nc.scalar.copy(
+                    out=grouped[:, a * PASS * PACK : (a + 1) * PASS * PACK].rearrange(
+                        "p (t m j) -> p m j t", t=PACK, j=PACK
+                    ),
+                    in_=raws[a][:].rearrange("p j (m t) -> p m j t", t=PACK),
+                )
+            w1_codes[b] = keep.tile([P, 2 * PASS], U32, name="w1_codes", tag=("w1_first", "slot_b")[b], align_bytes=64)
+            nc.vector.quantize_mx(out=w1_codes[b][:].bitcast(FP8X4), scales=w1_sc[:, b, :], in_=grouped[:])
+
+        w1_raws = load_w1(0)
+
+        tabs = []
+        for a in range(2):
+            tab = ring.tile([P, T], I32, name="tab", tag="tab_planes", align_bytes=64)
+            nc.sync.dma_start(out=tab[:], in_=tab_words[a].rearrange("p t i -> p (t i)").bitcast(I32))
+            tabs.append(tab)
+
+        wgs_t = keep.tile([P, PACK, S], F32, name="wgs_t")
+        wgs_rows = wgs.rearrange("(q t) j -> q t j", t=PACK)
+        expos = {}
+        pages = {}
+
+        def load_expo(i):
+            expos[i] = ring.tile([P, S], F32, name="expo_t", tag="expo_t", bufs=4)
+            nc.sync.dma_start(out=expos[i][:], in_=rows_of(expo, i))
+
+        def load_page(i):
+            pages[i] = ring.tile([P, T2], F32, name="page", bufs=7)
+            nc.sync.dma_start(out=pages[i][:], in_=rows_of(page0, i))
+
+        def load_wgs(t0, t1):
+            for q in (0, 2, 1, 3):
+                nc.sync.dma_start(out=wgs_t[32 * q : 32 * q + 32, t0:t1, :], in_=wgs_rows[:, t0:t1, :])
+
+        load_expo(0)
+        load_wgs(0, 1)
+        load_page(0)
+        load_expo(1)
+        load_wgs(1, PACK)
+        w1_later = load_w1(1)
+        load_expo(2)
+        load_page(1)
+        sv_t = keep.tile([P, 2, PACK], F32, name="sv_t")
+        nc.sync.dma_start(out=sv_t[:], in_=sv.rearrange("(b p t) -> p b t", b=2, t=PACK))
+        b4_t = keep.tile([P, N // P], F32, name="b4_t")
+        with nc.allow_non_contiguous_dma(reason="one bias value a partition"):
+            nc.sync.dma_start(out=b4_t[:], in_=b4.rearrange("(c p) -> p c", p=P))
+
+        w2_codes = keep.tile([P, 2, 2 * H], U8, name="w2_codes", align_bytes=64)
+        w2_sc = keep.tile([P, 2, H], U8, name="w2_sc", align_bytes=64)
+        nc.vector.tensor_copy(
+            out=w2_codes[:].bitcast(U16).rearrange("p a (b t m) -> p (a b) m t", b=2, t=PACK),
+            in_=w2_raw[:].bitcast(U16).rearrange("p a (b m t) -> p (a b) m t", b=2, t=PACK),
+        )
+        v_sc = []
+        for a in range(2):
+            plane = keep.tile([P, S], U8, name="v_sc%d" % a, align_bytes=64)
+            nc.vector.tensor_copy(plane[:], tab_sc[:, a, :].indirect(pick[:]))
+            v_sc.append(plane)
+        nc.vector.tensor_copy(
+            out=w2_sc[:].rearrange("p a (b t m) -> p (a b) t m", b=2, t=PACK),
+            in_=w2_sc_raw[:].rearrange("p a (b m t) -> p (a b) t m", b=2, t=PACK),
+        )
+        quantise_w1(0, w1_raws)
+        v_codes = keep.tile([P, 2, S], U32, name="v_codes", tag="grouped_v", align_bytes=64)
+        nc.vector.tensor_copy(v_codes[:, 0, :], tabs[0][:].bitcast(U32).indirect(pick[:]))
+        for h in range(2):
+            nc.vector.tensor_copy(v_codes[:, 1, half(h)], tabs[1][:].bitcast(U32).indirect(list_half(pick, h)))
+
+        def first_products(i, h):
+            b, t = divmod(i, PACK)
+            wind = psum.tile([P, BANK], F32, name="wind", tag="acc")
+            base = psum.tile([P, BANK], F32, name="base", tag="acc")
+            for a in range(2):
+                c2 = b * PASS + t * P
+                nc.tensor.matmul_mx(
+                    out=wind[:],
+                    lhsT=w2_codes[:, a, 2 * c2 : 2 * (c2 + P)].bitcast(FP4X4),
+                    lhsT_scale=w2_sc[:, a, c2 : c2 + P],
+                    rhs=v_codes[:, a, half(h)].bitcast(FP8X4),
+                    rhs_scale=v_sc[a][:, half(h)],
+                    start=(a == 0),
+                    stop=(a == 1),
+                )
+                c1 = a * PASS + t * P
+                nc.tensor.matmul_mx(
+                    out=base[:],
+                    lhsT=w1_codes[b][:, c1 : c1 + P].bitcast(FP8X4),
+                    lhsT_scale=w1_sc[:, b, c1 : c1 + P],
+                    rhs=v_codes[:, a, half(h)].bitcast(FP8X4),
+                    rhs_scale=v_sc[a][:, half(h)],
+                    start=(a == 0),
+                    stop=(a == 1),
+                )
+            return base, wind
+
+        hs = {}
+
+        def make_h(i):
+            t = i % PACK
+            hw = keep.tile([P, S], F32, name="hw", tag="slot_" + "abcadecd"[i], align_bytes=64)
+            hs[i] = hw
+            if PATH[i] == "G":
+                base_sb = ring.tile([P, S], F32, name="base_sb")
+                banks = [first_products(i, h) for h in range(2)]
+                for h in range(2):
+                    nc.scalar.copy(out=hw[:, half(h)], in_=banks[h][1][:])
+                for h in range(2):
+                    nc.scalar.copy(out=base_sb[:, half(h)], in_=banks[h][0][:])
+                nc.gpsimd.tensor_tensor(hw[:], hw[:], expos[i][:], MULT)
+                nc.gpsimd.tensor_tensor(hw[:], hw[:], base_sb[:], ADD)
+                nc.gpsimd.tensor_tensor(hw[:], hw[:], wgs_t[:, t, :], MULT)
+            elif PATH[i] == "M":
+                base_sb = ring.tile([P, S], F32, name="base_sb")
+                for h in range(2):
+                    base, wind = first_products(i, h)
+                    nc.vector.tensor_tensor(hw[:, half(h)], wind[:], expos[i][:, half(h)], MULT)
+                    nc.scalar.copy(out=base_sb[:, half(h)], in_=base[:])
+                nc.gpsimd.tensor_tensor(hw[:], hw[:], base_sb[:], ADD)
+                nc.gpsimd.tensor_tensor(hw[:], hw[:], wgs_t[:, t, :], MULT)
+            else:
+                for h in range(2):
+                    base, wind = first_products(i, h)
+                    nc.vector.tensor_tensor(hw[:, half(h)], wind[:], expos[i][:, half(h)], MULT)
+                    nc.vector.tensor_tensor(hw[:, half(h)], base[:], hw[:, half(h)], ADD)
+                    if PATH[i] == "H":
+                        nc.vector.tensor_tensor(hw[:, half(h)], hw[:, half(h)], wgs_t[:, t, half(h)], MULT)
+                        nc.vector.tensor_copy(pages[i][:].indirect(list_half(put, h)), hw[:, half(h)])
+
+        def scatter(i):
+            if PATH[i] in "GM":
+                nc.vector.tensor_copy(pages[i][:].indirect(put[:]), hs[i][:])
+            elif PATH[i] == "V":
+                nc.vector.tensor_tensor(pages[i][:].indirect(put[:]), hs[i][:], wgs_t[:, i % PACK, :], MULT)
+
+        page_planes = {}
+        x_planes = {}
+
+        def after_scatter(i):
+            b, t = divmod(i, PACK)
+            if t == 0:
+                page_planes[b] = ring.tile([P, PACK, T2], BF16, name="page_planes", tag="tab_planes", align_bytes=64)
+                x_planes[b] = keep.tile([P, PACK, M], BF16, name="x_planes", tag="tabsc_xplanes", align_bytes=64)
+            nc.sync.dma_start(out=rows_of(out_1, i), in_=pages[i][:])
+            xg = ring.tile([P, M], F32, name="xg", tag="xg", align_bytes=64)
+            if i < TILES - 1:
+                nc.vector.tensor_copy(xg[:], pages[i][:].indirect(read[:]))
+                nc.scalar.activation(out=x_planes[b][:, t, :], in_=xg[:], func=COPY, scale=sv_t[:, b, t : t + 1])
+                nc.scalar.copy(out=page_planes[b][:, t, :], in_=pages[i][:])
+            else:
+                for h in range(2):
+                    nc.vector.tensor_copy(xg[:, half(h)], pages[i][:].indirect(list_half(read, h)))
+                    nc.scalar.activation(
+                        out=x_planes[b][:, t, half(h)], in_=xg[:, half(h)], func=COPY, scale=sv_t[:, b, t : t + 1]
+                    )
+                for h in range(2):
+                    cols = slice(h * T2 // 2, (h + 1) * T2 // 2)
+                    nc.scalar.copy(out=page_planes[b][:, t, cols], in_=pages[i][:, cols])
+
+        def interleave(copy, dst, src):
+            copy(
+                out=dst.rearrange("p (c i t) -> p c t i", i=4, t=PACK),
+                in_=src.rearrange("p t (c i) -> p c t i", i=4),
+            )
+
+        x_codes = {}
+        x_sc = keep.tile([P, 2, M], U8, name="x_sc", align_bytes=64)
+
+        def weave_x(b, copy, h, inter):
+            interleave(copy, inter[:, h * BANK * PACK : (h + 1) * BANK * PACK], x_planes[b][:, :, half(h)])
+
+        def weave_page(b, c, copies):
+            inter = ring.tile([P, M * PACK], BF16, name="page_inter", tag="raw_inter", align_bytes=64)
+            for h in range(2):
+                c0 = c * 2 * BANK + h * BANK
+                interleave(copies[h], inter[:, h * BANK * PACK : (h + 1) * BANK * PACK], page_planes[b][:, :, c0 : c0 + BANK])
+            return inter
+
+        page_sc = [keep.tile([P, T2], U8, name="page_sc%d" % b, align_bytes=64) for b in range(2)]
+
+        def store_planes(b, c, inter, tag):
+            words = out_2[b].rearrange("p m t -> p (m t)").bitcast(I32)
+            cols = slice(c * 2 * BANK, (c + 1) * 2 * BANK)
+            codes = keep.tile([P, 2 * BANK], U32, name="page_codes", tag=tag, align_bytes=64)
+            nc.vector.quantize_mx(out=codes[:].bitcast(FP8X4), scales=page_sc[b][:, cols], in_=inter[:])
+            nc.sync.dma_start(out=words[:, cols], in_=codes[:].bitcast(I32))
+            if c == 1:
+                for q in range(4):
+                    nc.sync.dma_start(
+                        out=out_3[b, 4 * q : 4 * q + 4, :].bitcast(I32),
+                        in_=page_sc[b][32 * q : 32 * q + 4, :].bitcast(I32),
+                    )
+
+        w3_sc = keep.tile([P, 2 * N], U8, name="w3_sc", align_bytes=64)
+        w4_codes = keep.tile([P, 2, 2 * N], U8, name="w4_codes", align_bytes=64)
+
+        def round_w3():
+            grouped = keep.tile([P, 2 * N * PACK], BF16, name="w3_grouped", tag="grouped", align_bytes=64)
+            for a in range(2):
+                raw = ring.tile([P, PACK, N], F32, name="w3_raw", tag="raw_inter", align_bytes=64)
+                nc.sync.dma_start(out=raw[:], in_=w3[a * PASS : (a + 1) * PASS, :].rearrange("(p j) c -> p j c", j=PACK))
+                interleave(nc.scalar.copy, grouped[:, a * N * PACK : (a + 1) * N * PACK], raw[:])
+            nc.sync.dma_start(out=w4_codes[:].bitcast(I32), in_=w4_words.rearrange("a p c -> p a c").bitcast(I32))
+            return grouped
+
+        on_scalar = [nc.scalar.copy] * 2
+        make_h(0)
+        make_h(1)
+        for i in range(TILES):
+            if i + 2 < TILES:
+                make_h(i + 2)
+            scatter(i)
+            if i == 1:
+                quantise_w1(1, w1_later)
+                w3_grouped = round_w3()
+            if i == 3:
+                w3_codes = keep.tile([P, 2 * N], U32, name="w3_codes", tag="slot_a", align_bytes=64)
+                for c0, c1 in ((0, 512), (512, 2 * N)):
+                    nc.vector.quantize_mx(
+                        out=w3_codes[:, c0:c1].bitcast(FP8X4),
+                        scales=w3_sc[:, c0:c1],
+                        in_=w3_grouped[:, c0 * PACK : c1 * PACK],
+                    )
+            if i == 5:
+                x_codes[0] = keep.tile([P, M], U32, name="x_codes", tag="slot_e", align_bytes=64)
+                nc.vector.quantize_mx(out=x_codes[0][:].bitcast(FP8X4), scales=x_sc[:, 0, :], in_=x_inter[:])
+                page_inter_1 = weave_page(0, 1, on_scalar)
+            if i == 6:
+                store_planes(0, 0, page_inter_0, "slot_c")
+            if i + 2 < TILES:
+                load_page(i + 2)
+            if i + 3 < TILES:
+                load_expo(i + 3)
+            after_scatter(i)
+            if i == PACK - 1:
+                x_inter = ring.tile([P, M * PACK], BF16, name="x_inter", tag="raw_inter", align_bytes=64)
+                for h in range(2):
+                    weave_x(0, nc.scalar.copy, h, x_inter)
+            if i == PACK:
+                page_inter_0 = weave_page(0, 0, on_scalar)
+
+        def second_pass(bent, lin, a, c, h):
+            nc.tensor.matmul_mx(
+                out=bent[:],
+                lhsT=w4_codes[:, a, 2 * c * P : 2 * (c + 1) * P].bitcast(FP4X4),
+                lhsT_scale=w4_sc[:, a, c * P : (c + 1) * P],
+                rhs=x_codes[a][:, half(h)].bitcast(FP8X4),
+                rhs_scale=x_sc[:, a, half(h)],
+                start=(a == 0),
+                stop=(a == 1),
+            )
+            c3 = a * N + c * P
+            nc.tensor.matmul_mx(
+                out=lin[:],
+                lhsT=w3_codes[:, c3 : c3 + P].bitcast(FP8X4),
+                lhsT_scale=w3_sc[:, c3 : c3 + P],
+                rhs=x_codes[a][:, half(h)].bitcast(FP8X4),
+                rhs_scale=x_sc[:, a, half(h)],
+                start=(a == 0),
+                stop=(a == 1),
+            )
+
+        blocks = [(h, c) for h in range(2) for c in range(N // P)]
+        sums = {}
+
+        def open_block(h, c):
+            bent = psum.tile([P, BANK], F32, name="bent", tag="acc")
+            lin = psum.tile([P, BANK], F32, name="lin", tag="acc")
+            sums[h, c] = (bent, lin)
+            second_pass(bent, lin, 0, c, h)
+
+        for h, c in blocks[:4]:
+            open_block(h, c)
+        x_codes[1] = keep.tile([P, M], U32, name="x_codes", tag="x_last", align_bytes=64)
+        x_inter = ring.tile([P, M * PACK], BF16, name="x_inter", tag="raw_inter", align_bytes=64)
+        for h in range(2):
+            weave_x(1, nc.vector.tensor_copy, h, x_inter)
+            nc.vector.quantize_mx(
+                out=x_codes[1][:, half(h)].bitcast(FP8X4),
+                scales=x_sc[:, 1, half(h)],
+                in_=x_inter[:, h * BANK * PACK : (h + 1) * BANK * PACK],
+            )
+        store_planes(0, 1, page_inter_1, "slot_d")
+        page_inter_0 = weave_page(1, 0, on_scalar)
+        for n, (h, c) in enumerate(blocks):
+            bent, lin = sums[h, c]
+            second_pass(bent, lin, 1, c, h)
+            curve = ring.tile([P, BANK], F32, name="curve", tag="base_sb")
+            nc.scalar.activation(out=curve[:], in_=bent[:], func=TANH, bias=b4_t[:, c : c + 1])
+            y = ring.tile([P, BANK], F32, name="y", tag="expo_t", bufs=4)
+            nc.vector.tensor_tensor(y[:], lin[:], curve[:], ADD)
+            nc.sync.dma_start(out=out_0[c * P : (c + 1) * P, half(h)], in_=y[:])
+            if n + 4 < len(blocks):
+                open_block(*blocks[n + 4])
+        store_planes(1, 0, page_inter_0, "pc_0")
+        store_planes(1, 1, weave_page(1, 1, [nc.vector.tensor_copy] * 2), "pc_1")

@@ -23,7 +23,7 @@ PACK = 4
 PASS = P * PACK
 BANK = 512
 TILES = H // P
-PATH = "HGGGGGGG"
+PATH = "HVVVVVVV"
 
 
 def tile_list_snow_cell_page_kernel(
@@ -55,9 +55,8 @@ def tile_list_snow_cell_page_kernel(
         nc.sync.dma_start(read[:], offs3)
 
         def load_scale_rows(tile, src):
-            nc.vector.memset(tile[:].bitcast(I32), 0)
             for q in range(4):
-                nc.gpsimd.dma_start(
+                nc.sync.dma_start(
                     out=tile[32 * q : 32 * q + 4, :, :].bitcast(I32),
                     in_=src[:, 4 * q : 4 * q + 4, :].rearrange("a r c -> r a c").bitcast(I32),
                 )
@@ -65,9 +64,13 @@ def tile_list_snow_cell_page_kernel(
         tab_sc = keep.tile([P, 2, T], U8, name="tab_sc", tag="tabsc_xplanes", align_bytes=64)
         w2_sc_raw = keep.tile([P, 2, H], U8, name="w2_sc_raw", tag="w1_first", align_bytes=64)
         w4_sc = keep.tile([P, 2, N], U8, name="w4_sc", align_bytes=64)
-        load_scale_rows(tab_sc, tab_scales)
-        load_scale_rows(w2_sc_raw, w2_scales)
-        load_scale_rows(w4_sc, w4_scales)
+        for plane in (tab_sc, w2_sc_raw, w4_sc):
+            nc.vector.memset(plane[:].bitcast(I32), 0)
+        sv_t = keep.tile([P, 2, PACK], F32, name="sv_t")
+        nc.sync.dma_start(out=sv_t[:], in_=sv.rearrange("(b p t) -> p b t", b=2, t=PACK))
+        b4_t = keep.tile([P, N // P], F32, name="b4_t")
+        with nc.allow_non_contiguous_dma(reason="one bias value a partition"):
+            nc.sync.dma_start(out=b4_t[:], in_=b4.rearrange("(c p) -> p c", p=P))
 
         w2_raw = ring.tile([P, 2, 2 * H], U8, name="w2_raw", tag="xg", align_bytes=64)
         nc.sync.dma_start(out=w2_raw[:].bitcast(I32), in_=w2_words.rearrange("a p c -> p a c").bitcast(I32))
@@ -97,6 +100,8 @@ def tile_list_snow_cell_page_kernel(
             nc.vector.quantize_mx(out=w1_codes[b][:].bitcast(FP8X4), scales=w1_sc[:, b, :], in_=grouped[:])
 
         w1_raws = load_w1(0)
+        load_scale_rows(w2_sc_raw, w2_scales)
+        load_scale_rows(tab_sc, tab_scales)
 
         tabs = []
         for a in range(2):
@@ -121,19 +126,17 @@ def tile_list_snow_cell_page_kernel(
             for q in (0, 2, 1, 3):
                 nc.sync.dma_start(out=wgs_t[32 * q : 32 * q + 32, t0:t1, :], in_=wgs_rows[:, t0:t1, :])
 
-        load_expo(0)
+        expos[0] = ring.tile([P, S], F32, name="expo_t", tag="expo_t", bufs=4)
+        nc.sync.dma_start(out=expos[0][:, half(0)], in_=rows_of(expo, 0)[:, half(0)])
         load_wgs(0, 1)
         load_page(0)
+        nc.sync.dma_start(out=expos[0][:, half(1)], in_=rows_of(expo, 0)[:, half(1)])
         load_expo(1)
         load_wgs(1, PACK)
         w1_later = load_w1(1)
         load_expo(2)
         load_page(1)
-        sv_t = keep.tile([P, 2, PACK], F32, name="sv_t")
-        nc.sync.dma_start(out=sv_t[:], in_=sv.rearrange("(b p t) -> p b t", b=2, t=PACK))
-        b4_t = keep.tile([P, N // P], F32, name="b4_t")
-        with nc.allow_non_contiguous_dma(reason="one bias value a partition"):
-            nc.sync.dma_start(out=b4_t[:], in_=b4.rearrange("(c p) -> p c", p=P))
+        load_scale_rows(w4_sc, w4_scales)
 
         w2_codes = keep.tile([P, 2, 2 * H], U8, name="w2_codes", align_bytes=64)
         w2_sc = keep.tile([P, 2, H], U8, name="w2_sc", align_bytes=64)
@@ -141,15 +144,15 @@ def tile_list_snow_cell_page_kernel(
             out=w2_codes[:].bitcast(U16).rearrange("p a (b t m) -> p (a b) m t", b=2, t=PACK),
             in_=w2_raw[:].bitcast(U16).rearrange("p a (b m t) -> p (a b) m t", b=2, t=PACK),
         )
+        nc.vector.tensor_copy(
+            out=w2_sc[:].rearrange("p a (b t m) -> p (a b) t m", b=2, t=PACK),
+            in_=w2_sc_raw[:].rearrange("p a (b m t) -> p (a b) t m", b=2, t=PACK),
+        )
         v_sc = []
         for a in range(2):
             plane = keep.tile([P, S], U8, name="v_sc%d" % a, align_bytes=64)
             nc.vector.tensor_copy(plane[:], tab_sc[:, a, :].indirect(pick[:]))
             v_sc.append(plane)
-        nc.vector.tensor_copy(
-            out=w2_sc[:].rearrange("p a (b t m) -> p (a b) t m", b=2, t=PACK),
-            in_=w2_sc_raw[:].rearrange("p a (b m t) -> p (a b) t m", b=2, t=PACK),
-        )
         quantise_w1(0, w1_raws)
         v_codes = keep.tile([P, 2, S], U32, name="v_codes", tag="grouped_v", align_bytes=64)
         nc.vector.tensor_copy(v_codes[:, 0, :], tabs[0][:].bitcast(U32).indirect(pick[:]))
@@ -207,14 +210,20 @@ def tile_list_snow_cell_page_kernel(
                     nc.scalar.copy(out=base_sb[:, half(h)], in_=base[:])
                 nc.gpsimd.tensor_tensor(hw[:], hw[:], base_sb[:], ADD)
                 nc.gpsimd.tensor_tensor(hw[:], hw[:], wgs_t[:, t, :], MULT)
-            else:
+            elif PATH[i] == "H":
                 for h in range(2):
                     base, wind = first_products(i, h)
                     nc.vector.tensor_tensor(hw[:, half(h)], wind[:], expos[i][:, half(h)], MULT)
                     nc.vector.tensor_tensor(hw[:, half(h)], base[:], hw[:, half(h)], ADD)
-                    if PATH[i] == "H":
-                        nc.vector.tensor_tensor(hw[:, half(h)], hw[:, half(h)], wgs_t[:, t, half(h)], MULT)
-                        nc.vector.tensor_copy(pages[i][:].indirect(list_half(put, h)), hw[:, half(h)])
+                    nc.vector.tensor_tensor(
+                        pages[i][:].indirect(list_half(put, h)), hw[:, half(h)], wgs_t[:, t, half(h)], MULT
+                    )
+            else:
+                banks = [first_products(i, h) for h in range(2)]
+                for h in range(2):
+                    nc.vector.tensor_tensor(hw[:, half(h)], banks[h][1][:], expos[i][:, half(h)], MULT)
+                for h in range(2):
+                    nc.vector.tensor_tensor(hw[:, half(h)], banks[h][0][:], hw[:, half(h)], ADD)
 
         def scatter(i):
             if PATH[i] in "GM":
@@ -296,9 +305,9 @@ def tile_list_snow_cell_page_kernel(
         make_h(0)
         make_h(1)
         for i in range(TILES):
+            scatter(i)
             if i + 2 < TILES:
                 make_h(i + 2)
-            scatter(i)
             if i == 1:
                 quantise_w1(1, w1_later)
                 w3_grouped = round_w3()

@@ -23,7 +23,7 @@ PACK = 4
 PASS = P * PACK
 BANK = 512
 TILES = H // P
-PATH = "HVVVVVVV"
+PATH = "HGGGGGGG"
 
 
 def tile_list_snow_cell_page_kernel(
@@ -57,11 +57,11 @@ def tile_list_snow_cell_page_kernel(
         def load_scale_rows(tile, src):
             for q in range(4):
                 nc.sync.dma_start(
-                    out=tile[32 * q : 32 * q + 4, :, :].bitcast(I32),
-                    in_=src[:, 4 * q : 4 * q + 4, :].rearrange("a r c -> r a c").bitcast(I32),
+                    out=tile[q:P:32, :, :].bitcast(I32),
+                    in_=src.rearrange("a (g r) c -> r g a c", r=4)[q].bitcast(I32),
                 )
 
-        tab_sc = keep.tile([P, 2, T], U8, name="tab_sc", tag="tabsc_xplanes", align_bytes=64)
+        tab_sc = keep.tile([P, 2, T], U8, name="tab_sc", tag="tabsc_grouped", align_bytes=64)
         w2_sc_raw = keep.tile([P, 2, H], U8, name="w2_sc_raw", tag="w1_first", align_bytes=64)
         w4_sc = keep.tile([P, 2, N], U8, name="w4_sc", align_bytes=64)
         for plane in (tab_sc, w2_sc_raw, w4_sc):
@@ -73,39 +73,41 @@ def tile_list_snow_cell_page_kernel(
             nc.sync.dma_start(out=b4_t[:], in_=b4.rearrange("(c p) -> p c", p=P))
 
         w2_raw = ring.tile([P, 2, 2 * H], U8, name="w2_raw", tag="xg", align_bytes=64)
-        nc.sync.dma_start(out=w2_raw[:].bitcast(I32), in_=w2_words.rearrange("a p c -> p a c").bitcast(I32))
+        for a in range(2):
+            nc.sync.dma_start(out=w2_raw[:, a, :].bitcast(I32), in_=w2_words[a].bitcast(I32))
 
         w1_codes = {}
         w1_sc = keep.tile([P, 2, 2 * PASS], U8, name="w1_sc", align_bytes=64)
 
-        def load_w1(b):
-            raws = []
-            for a in range(2):
-                raw = ring.tile([P, PACK, PASS], F32, name="w1_raw", tag="raw_inter", align_bytes=64)
-                src = w1[a * PASS : (a + 1) * PASS, b * PASS : (b + 1) * PASS]
-                nc.sync.dma_start(out=raw[:], in_=src.rearrange("(p j) c -> p j c", j=PACK))
-                raws.append(raw)
-            return raws
+        def load_w1(raw, a, b):
+            src = w1[a * PASS : (a + 1) * PASS, b * PASS : (b + 1) * PASS]
+            nc.sync.dma_start(out=raw, in_=src.rearrange("(p j) c -> p j c", j=PACK))
+            return raw
 
-        def quantise_w1(b, raws):
-            grouped = keep.tile([P, 2 * PASS * PACK], BF16, name="w1_grouped", tag=("grouped_v", "grouped")[b], align_bytes=64)
+        def round_w1(b, raws):
+            grouped = keep.tile([P, 2 * PASS * PACK], BF16, name="w1_grouped", tag=("grouped_v", "tabsc_grouped")[b], align_bytes=64)
             for a in range(2):
                 nc.scalar.copy(
                     out=grouped[:, a * PASS * PACK : (a + 1) * PASS * PACK].rearrange(
-                        "p (t m j) -> p m j t", t=PACK, j=PACK
+                        "p (t m j) -> p m t j", t=PACK, j=PACK
                     ),
-                    in_=raws[a][:].rearrange("p j (m t) -> p m j t", t=PACK),
+                    in_=raws[a].rearrange("p j (m t) -> p m t j", t=PACK),
                 )
-            w1_codes[b] = keep.tile([P, 2 * PASS], U32, name="w1_codes", tag=("w1_first", "slot_b")[b], align_bytes=64)
+            return grouped
+
+        def quantise_w1(b, grouped):
+            w1_codes[b] = keep.tile([P, 2 * PASS], U32, name="w1_codes", tag=("w1_first", "slot_1")[b], align_bytes=64)
             nc.vector.quantize_mx(out=w1_codes[b][:].bitcast(FP8X4), scales=w1_sc[:, b, :], in_=grouped[:])
 
-        w1_raws = load_w1(0)
+        w1_first = [ring.tile([P, PACK, PASS], F32, name="w1_raw", tag="raw_inter", align_bytes=64) for a in range(2)]
+        w1_raws = [load_w1(w1_first[0][:], 0, 0)]
         load_scale_rows(w2_sc_raw, w2_scales)
         load_scale_rows(tab_sc, tab_scales)
+        w1_raws.append(load_w1(w1_first[1][:], 1, 0))
 
         tabs = []
         for a in range(2):
-            tab = ring.tile([P, T], I32, name="tab", tag="tab_planes", align_bytes=64)
+            tab = keep.tile([P, T], I32, name="tab", tag="tab_%d" % a, align_bytes=64)
             nc.sync.dma_start(out=tab[:], in_=tab_words[a].rearrange("p t i -> p (t i)").bitcast(I32))
             tabs.append(tab)
 
@@ -126,23 +128,26 @@ def tile_list_snow_cell_page_kernel(
             for q in (0, 2, 1, 3):
                 nc.sync.dma_start(out=wgs_t[32 * q : 32 * q + 32, t0:t1, :], in_=wgs_rows[:, t0:t1, :])
 
-        expos[0] = ring.tile([P, S], F32, name="expo_t", tag="expo_t", bufs=4)
-        nc.sync.dma_start(out=expos[0][:, half(0)], in_=rows_of(expo, 0)[:, half(0)])
+        load_expo(0)
         load_wgs(0, 1)
-        load_page(0)
-        nc.sync.dma_start(out=expos[0][:, half(1)], in_=rows_of(expo, 0)[:, half(1)])
         load_expo(1)
-        load_wgs(1, PACK)
-        w1_later = load_w1(1)
-        load_expo(2)
+        load_page(0)
+        w1_rest = [
+            keep.tile([P, PACK, PASS], F32, name="w1_rest", tag=("tab_0", "x_planes")[a], align_bytes=64) for a in range(2)
+        ]
+        w1_later = [load_w1(w1_rest[a][:], a, 1) for a in range(2)]
+        load_wgs(1, 2)
         load_page(1)
+        load_expo(2)
+        load_wgs(2, PACK)
+        load_expo(3)
         load_scale_rows(w4_sc, w4_scales)
 
         w2_codes = keep.tile([P, 2, 2 * H], U8, name="w2_codes", align_bytes=64)
         w2_sc = keep.tile([P, 2, H], U8, name="w2_sc", align_bytes=64)
         nc.vector.tensor_copy(
-            out=w2_codes[:].bitcast(U16).rearrange("p a (b t m) -> p (a b) m t", b=2, t=PACK),
-            in_=w2_raw[:].bitcast(U16).rearrange("p a (b m t) -> p (a b) m t", b=2, t=PACK),
+            out=w2_codes[:].bitcast(U16).rearrange("p a (b t m) -> p (a b) t m", b=2, t=PACK),
+            in_=w2_raw[:].bitcast(U16).rearrange("p a (b m t) -> p (a b) t m", b=2, t=PACK),
         )
         nc.vector.tensor_copy(
             out=w2_sc[:].rearrange("p a (b t m) -> p (a b) t m", b=2, t=PACK),
@@ -153,7 +158,7 @@ def tile_list_snow_cell_page_kernel(
             plane = keep.tile([P, S], U8, name="v_sc%d" % a, align_bytes=64)
             nc.vector.tensor_copy(plane[:], tab_sc[:, a, :].indirect(pick[:]))
             v_sc.append(plane)
-        quantise_w1(0, w1_raws)
+        quantise_w1(0, round_w1(0, w1_raws))
         v_codes = keep.tile([P, 2, S], U32, name="v_codes", tag="grouped_v", align_bytes=64)
         nc.vector.tensor_copy(v_codes[:, 0, :], tabs[0][:].bitcast(U32).indirect(pick[:]))
         for h in range(2):
@@ -190,10 +195,10 @@ def tile_list_snow_cell_page_kernel(
 
         def make_h(i):
             t = i % PACK
-            hw = keep.tile([P, S], F32, name="hw", tag="slot_" + "abcadecd"[i], align_bytes=64)
+            hw = keep.tile([P, S], F32, name="hw", tag="slot_%d" % i, align_bytes=64)
             hs[i] = hw
             if PATH[i] == "G":
-                base_sb = ring.tile([P, S], F32, name="base_sb")
+                base_sb = ring.tile([P, S], F32, name="base_sb", tag="base_sb", bufs=3)
                 banks = [first_products(i, h) for h in range(2)]
                 for h in range(2):
                     nc.scalar.copy(out=hw[:, half(h)], in_=banks[h][1][:])
@@ -203,30 +208,24 @@ def tile_list_snow_cell_page_kernel(
                 nc.gpsimd.tensor_tensor(hw[:], hw[:], base_sb[:], ADD)
                 nc.gpsimd.tensor_tensor(hw[:], hw[:], wgs_t[:, t, :], MULT)
             elif PATH[i] == "M":
-                base_sb = ring.tile([P, S], F32, name="base_sb")
+                base_sb = ring.tile([P, S], F32, name="base_sb", tag="base_sb", bufs=3)
                 for h in range(2):
                     base, wind = first_products(i, h)
                     nc.vector.tensor_tensor(hw[:, half(h)], wind[:], expos[i][:, half(h)], MULT)
                     nc.scalar.copy(out=base_sb[:, half(h)], in_=base[:])
                 nc.gpsimd.tensor_tensor(hw[:], hw[:], base_sb[:], ADD)
                 nc.gpsimd.tensor_tensor(hw[:], hw[:], wgs_t[:, t, :], MULT)
-            elif PATH[i] == "H":
-                for h in range(2):
-                    base, wind = first_products(i, h)
-                    nc.vector.tensor_tensor(hw[:, half(h)], wind[:], expos[i][:, half(h)], MULT)
-                    nc.vector.tensor_tensor(hw[:, half(h)], base[:], hw[:, half(h)], ADD)
-                    nc.vector.tensor_tensor(
-                        pages[i][:].indirect(list_half(put, h)), hw[:, half(h)], wgs_t[:, t, half(h)], MULT
-                    )
             else:
                 banks = [first_products(i, h) for h in range(2)]
                 for h in range(2):
                     nc.vector.tensor_tensor(hw[:, half(h)], banks[h][1][:], expos[i][:, half(h)], MULT)
                 for h in range(2):
                     nc.vector.tensor_tensor(hw[:, half(h)], banks[h][0][:], hw[:, half(h)], ADD)
+                if PATH[i] == "H":
+                    nc.vector.tensor_tensor(hw[:], hw[:], wgs_t[:, t, :], MULT)
 
         def scatter(i):
-            if PATH[i] in "GM":
+            if PATH[i] in "GMH":
                 nc.vector.tensor_copy(pages[i][:].indirect(put[:]), hs[i][:])
             elif PATH[i] == "V":
                 nc.vector.tensor_tensor(pages[i][:].indirect(put[:]), hs[i][:], wgs_t[:, i % PACK, :], MULT)
@@ -234,11 +233,11 @@ def tile_list_snow_cell_page_kernel(
         page_planes = {}
         x_planes = {}
 
-        def after_scatter(i):
+        def after_scatter(i, last_inter):
             b, t = divmod(i, PACK)
             if t == 0:
-                page_planes[b] = ring.tile([P, PACK, T2], BF16, name="page_planes", tag="tab_planes", align_bytes=64)
-                x_planes[b] = keep.tile([P, PACK, M], BF16, name="x_planes", tag="tabsc_xplanes", align_bytes=64)
+                page_planes[b] = keep.tile([P, PACK, T2], BF16, name="page_planes", tag="tab_%d" % b, align_bytes=64)
+                x_planes[b] = keep.tile([P, PACK, M], BF16, name="x_planes", tag="x_planes", align_bytes=64)
             nc.sync.dma_start(out=rows_of(out_1, i), in_=pages[i][:])
             xg = ring.tile([P, M], F32, name="xg", tag="xg", align_bytes=64)
             if i < TILES - 1:
@@ -249,11 +248,14 @@ def tile_list_snow_cell_page_kernel(
                 for h in range(2):
                     nc.vector.tensor_copy(xg[:, half(h)], pages[i][:].indirect(list_half(read, h)))
                     nc.scalar.activation(
-                        out=x_planes[b][:, t, half(h)], in_=xg[:, half(h)], func=COPY, scale=sv_t[:, b, t : t + 1]
+                        out=last_inter[:].rearrange("p (m t) -> p m t", t=PACK)[:, half(h), t],
+                        in_=xg[:, half(h)],
+                        func=COPY,
+                        scale=sv_t[:, b, t : t + 1],
                     )
-                for h in range(2):
                     cols = slice(h * T2 // 2, (h + 1) * T2 // 2)
                     nc.scalar.copy(out=page_planes[b][:, t, cols], in_=pages[i][:, cols])
+
 
         def interleave(copy, dst, src):
             copy(
@@ -285,15 +287,15 @@ def tile_list_snow_cell_page_kernel(
             if c == 1:
                 for q in range(4):
                     nc.sync.dma_start(
-                        out=out_3[b, 4 * q : 4 * q + 4, :].bitcast(I32),
-                        in_=page_sc[b][32 * q : 32 * q + 4, :].bitcast(I32),
+                        out=out_3[b].rearrange("(g r) c -> r g c", r=4)[q].bitcast(I32),
+                        in_=page_sc[b][q:P:32, :].bitcast(I32),
                     )
 
         w3_sc = keep.tile([P, 2 * N], U8, name="w3_sc", align_bytes=64)
         w4_codes = keep.tile([P, 2, 2 * N], U8, name="w4_codes", align_bytes=64)
 
         def round_w3():
-            grouped = keep.tile([P, 2 * N * PACK], BF16, name="w3_grouped", tag="grouped", align_bytes=64)
+            grouped = keep.tile([P, 2 * N * PACK], BF16, name="w3_grouped", tag="tabsc_grouped", align_bytes=64)
             for a in range(2):
                 raw = ring.tile([P, PACK, N], F32, name="w3_raw", tag="raw_inter", align_bytes=64)
                 nc.sync.dma_start(out=raw[:], in_=w3[a * PASS : (a + 1) * PASS, :].rearrange("(p j) c -> p j c", j=PACK))
@@ -302,17 +304,21 @@ def tile_list_snow_cell_page_kernel(
             return grouped
 
         on_scalar = [nc.scalar.copy] * 2
+        last_inter = None
         make_h(0)
         make_h(1)
+        make_h(2)
         for i in range(TILES):
+            if i + 4 < TILES:
+                load_expo(i + 4)
             scatter(i)
-            if i + 2 < TILES:
-                make_h(i + 2)
+            if i == 0:
+                w1_grouped = round_w1(1, w1_later)
             if i == 1:
-                quantise_w1(1, w1_later)
+                quantise_w1(1, w1_grouped)
                 w3_grouped = round_w3()
-            if i == 3:
-                w3_codes = keep.tile([P, 2 * N], U32, name="w3_codes", tag="slot_a", align_bytes=64)
+            if i == 4:
+                w3_codes = keep.tile([P, 2 * N], U32, name="w3_codes", tag="slot_4", align_bytes=64)
                 for c0, c1 in ((0, 512), (512, 2 * N)):
                     nc.vector.quantize_mx(
                         out=w3_codes[:, c0:c1].bitcast(FP8X4),
@@ -320,16 +326,25 @@ def tile_list_snow_cell_page_kernel(
                         in_=w3_grouped[:, c0 * PACK : c1 * PACK],
                     )
             if i == 5:
-                x_codes[0] = keep.tile([P, M], U32, name="x_codes", tag="slot_e", align_bytes=64)
+                x_codes[0] = keep.tile([P, M], U32, name="x_codes", tag="slot_5", align_bytes=64)
                 nc.vector.quantize_mx(out=x_codes[0][:].bitcast(FP8X4), scales=x_sc[:, 0, :], in_=x_inter[:])
                 page_inter_1 = weave_page(0, 1, on_scalar)
             if i == 6:
-                store_planes(0, 0, page_inter_0, "slot_c")
+                store_planes(0, 0, page_inter_0, "slot_6")
+            if i + 3 < TILES:
+                make_h(i + 3)
             if i + 2 < TILES:
                 load_page(i + 2)
-            if i + 3 < TILES:
-                load_expo(i + 3)
-            after_scatter(i)
+            after_scatter(i, last_inter)
+            if i == TILES - 2:
+                last_inter = ring.tile([P, M * PACK], BF16, name="last_inter", tag="raw_inter", align_bytes=64)
+                for h in range(2):
+                    nc.scalar.copy(
+                        out=last_inter[:, h * BANK * PACK : (h + 1) * BANK * PACK].rearrange(
+                            "p (c i t) -> p c t i", i=4, t=PACK
+                        )[:, :, 0 : PACK - 1, :],
+                        in_=x_planes[1][:, 0 : PACK - 1, half(h)].rearrange("p t (c i) -> p c t i", i=4),
+                    )
             if i == PACK - 1:
                 x_inter = ring.tile([P, M * PACK], BF16, name="x_inter", tag="raw_inter", align_bytes=64)
                 for h in range(2):
@@ -369,26 +384,24 @@ def tile_list_snow_cell_page_kernel(
 
         for h, c in blocks[:4]:
             open_block(h, c)
-        x_codes[1] = keep.tile([P, M], U32, name="x_codes", tag="x_last", align_bytes=64)
-        x_inter = ring.tile([P, M * PACK], BF16, name="x_inter", tag="raw_inter", align_bytes=64)
+        x_codes[1] = keep.tile([P, M], U32, name="x_codes", tag="slot_0", align_bytes=64)
         for h in range(2):
-            weave_x(1, nc.vector.tensor_copy, h, x_inter)
             nc.vector.quantize_mx(
                 out=x_codes[1][:, half(h)].bitcast(FP8X4),
                 scales=x_sc[:, 1, half(h)],
-                in_=x_inter[:, h * BANK * PACK : (h + 1) * BANK * PACK],
+                in_=last_inter[:, h * BANK * PACK : (h + 1) * BANK * PACK],
             )
-        store_planes(0, 1, page_inter_1, "slot_d")
-        page_inter_0 = weave_page(1, 0, on_scalar)
+        store_planes(0, 1, page_inter_1, "slot_7")
+        store_planes(1, 0, weave_page(1, 0, [nc.vector.tensor_copy, nc.vector.tensor_copy]), "slot_2")
         for n, (h, c) in enumerate(blocks):
             bent, lin = sums[h, c]
             second_pass(bent, lin, 1, c, h)
-            curve = ring.tile([P, BANK], F32, name="curve", tag="base_sb")
+            curve = ring.tile([P, BANK], F32, name="curve", tag="base_sb", bufs=3)
             nc.scalar.activation(out=curve[:], in_=bent[:], func=TANH, bias=b4_t[:, c : c + 1])
             y = ring.tile([P, BANK], F32, name="y", tag="expo_t", bufs=4)
             nc.vector.tensor_tensor(y[:], lin[:], curve[:], ADD)
             nc.sync.dma_start(out=out_0[c * P : (c + 1) * P, half(h)], in_=y[:])
             if n + 4 < len(blocks):
                 open_block(*blocks[n + 4])
-        store_planes(1, 0, page_inter_0, "pc_0")
-        store_planes(1, 1, weave_page(1, 1, [nc.vector.tensor_copy] * 2), "pc_1")
+            if n == 2:
+                store_planes(1, 1, weave_page(1, 1, [nc.vector.tensor_copy, nc.scalar.copy]), "slot_3")

@@ -19,11 +19,18 @@ COPY = mybir.ActivationFunctionType.Copy
 TANH = mybir.ActivationFunctionType.Tanh
 
 P = 128
+QUAD = 32
 PACK = 4
 PASS = P * PACK
 BANK = 512
 TILES = H // P
-PATH = "HGGGGGGG"
+LAST = TILES - 1
+ALIGN = 64
+H_AHEAD = 3
+EXPO_BUFS = H_AHEAD + 1
+PAGE_AHEAD = 2
+PAGE_BUFS = 6
+OPEN_BLOCKS = 4
 
 
 def tile_list_snow_cell_page_kernel(
@@ -41,11 +48,14 @@ def tile_list_snow_cell_page_kernel(
             b, t = divmod(i, PACK)
             return mat[b * PASS : (b + 1) * PASS, :].rearrange("(p t) c -> p t c", t=PACK)[:, t, :]
 
-        def half(h):
-            return slice(h * BANK, (h + 1) * BANK)
+        def half(hf):
+            return slice(hf * BANK, (hf + 1) * BANK)
 
-        def list_half(lst, h):
-            return lst[:, h * (BANK // 16) : (h + 1) * (BANK // 16)]
+        def list_half(lst, hf):
+            return lst[:, hf * (BANK // 16) : (hf + 1) * (BANK // 16)]
+
+        def h_slot(i):
+            return "h_slot_%d" % i
 
         pick = lists.tile([P, S // 16], U16, name="pick")
         put = lists.tile([P, S // 16], U16, name="put")
@@ -54,60 +64,58 @@ def tile_list_snow_cell_page_kernel(
         nc.sync.dma_start(put[:], offs2)
         nc.sync.dma_start(read[:], offs3)
 
-        def load_scale_rows(tile, src):
-            for q in range(4):
+        def load_scale_rows(planes, src):
+            for s in range(4):
                 nc.sync.dma_start(
-                    out=tile[q:P:32, :, :].bitcast(I32),
-                    in_=src.rearrange("a (g r) c -> r g a c", r=4)[q].bitcast(I32),
+                    out=planes[s:P:QUAD, :, :].bitcast(I32),
+                    in_=src.rearrange("a (g row) c -> row g a c", row=4)[s].bitcast(I32),
                 )
 
-        tab_sc = keep.tile([P, 2, T], U8, name="tab_sc", tag="tabsc_grouped", align_bytes=64)
-        w2_sc_raw = keep.tile([P, 2, H], U8, name="w2_sc_raw", tag="w1_first", align_bytes=64)
-        w4_sc = keep.tile([P, 2, N], U8, name="w4_sc", align_bytes=64)
-        for plane in (tab_sc, w2_sc_raw, w4_sc):
-            nc.vector.memset(plane[:].bitcast(I32), 0)
-        sv_t = keep.tile([P, 2, PACK], F32, name="sv_t")
-        nc.sync.dma_start(out=sv_t[:], in_=sv.rearrange("(b p t) -> p b t", b=2, t=PACK))
-        b4_t = keep.tile([P, N // P], F32, name="b4_t")
-        with nc.allow_non_contiguous_dma(reason="one bias value a partition"):
-            nc.sync.dma_start(out=b4_t[:], in_=b4.rearrange("(c p) -> p c", p=P))
+        tab_sc = keep.tile([P, 2, T], U8, name="tab_sc", tag="chain", align_bytes=ALIGN)
+        w2_sc_raw = keep.tile([P, 2, H], U8, name="w2_sc_raw", align_bytes=ALIGN)
+        w4_sc = keep.tile([P, 2, N], U8, name="w4_sc", align_bytes=ALIGN)
+        for planes in (w2_sc_raw, tab_sc, w4_sc):
+            nc.vector.memset(planes[:].bitcast(I32), 0)
 
-        w2_raw = ring.tile([P, 2, 2 * H], U8, name="w2_raw", tag="xg", align_bytes=64)
+        w2_raw = ring.tile([P, 2, 2 * H], U8, name="w2_raw", tag="picked", align_bytes=ALIGN)
         for a in range(2):
-            nc.sync.dma_start(out=w2_raw[:, a, :].bitcast(I32), in_=w2_words[a].bitcast(I32))
+            for b in range(2):
+                cols = slice(b * 2 * PASS, (b + 1) * 2 * PASS)
+                nc.sync.dma_start(out=w2_raw[:, a, cols].bitcast(I32), in_=w2_words[a][:, cols].bitcast(I32))
 
         w1_codes = {}
-        w1_sc = keep.tile([P, 2, 2 * PASS], U8, name="w1_sc", align_bytes=64)
+        w1_sc = keep.tile([P, 2, 2 * PASS], U8, name="w1_sc", align_bytes=ALIGN)
 
         def load_w1(raw, a, b):
             src = w1[a * PASS : (a + 1) * PASS, b * PASS : (b + 1) * PASS]
-            nc.sync.dma_start(out=raw, in_=src.rearrange("(p j) c -> p j c", j=PACK))
-            return raw
+            nc.sync.dma_start(out=raw[:], in_=src.rearrange("(p j) c -> p j c", j=PACK))
 
-        def round_w1(b, raws):
-            grouped = keep.tile([P, 2 * PASS * PACK], BF16, name="w1_grouped", tag=("grouped_v", "tabsc_grouped")[b], align_bytes=64)
+        def round_w1(raws, tag):
+            rounded = keep.tile([P, 2 * PASS * PACK], BF16, name="w1_rounded", tag=tag, align_bytes=ALIGN)
             for a in range(2):
                 nc.scalar.copy(
-                    out=grouped[:, a * PASS * PACK : (a + 1) * PASS * PACK].rearrange(
+                    out=rounded[:, a * PASS * PACK : (a + 1) * PASS * PACK].rearrange(
                         "p (t m j) -> p m t j", t=PACK, j=PACK
                     ),
-                    in_=raws[a].rearrange("p j (m t) -> p m t j", t=PACK),
+                    in_=raws[a][:].rearrange("p j (m t) -> p m t j", t=PACK),
                 )
-            return grouped
+            return rounded
 
-        def quantise_w1(b, grouped):
-            w1_codes[b] = keep.tile([P, 2 * PASS], U32, name="w1_codes", tag=("w1_first", "slot_1")[b], align_bytes=64)
-            nc.vector.quantize_mx(out=w1_codes[b][:].bitcast(FP8X4), scales=w1_sc[:, b, :], in_=grouped[:])
+        def quantise_w1(b, rounded, tag):
+            w1_codes[b] = keep.tile([P, 2 * PASS], U32, name="w1_codes", tag=tag, align_bytes=ALIGN)
+            nc.vector.quantize_mx(out=w1_codes[b][:].bitcast(FP8X4), scales=w1_sc[:, b, :], in_=rounded[:])
 
-        w1_first = [ring.tile([P, PACK, PASS], F32, name="w1_raw", tag="raw_inter", align_bytes=64) for a in range(2)]
-        w1_raws = [load_w1(w1_first[0][:], 0, 0)]
+        w1_first = [ring.tile([P, PACK, PASS], F32, name="w1_first", tag="stage", align_bytes=ALIGN) for a in range(2)]
+        sv_t = keep.tile([P, 2, PACK], F32, name="sv_t")
+        nc.sync.dma_start(out=sv_t[:], in_=sv.rearrange("(b p t) -> p b t", b=2, t=PACK))
         load_scale_rows(w2_sc_raw, w2_scales)
         load_scale_rows(tab_sc, tab_scales)
-        w1_raws.append(load_w1(w1_first[1][:], 1, 0))
+        for a in range(2):
+            load_w1(w1_first[a], a, 0)
 
         tabs = []
         for a in range(2):
-            tab = keep.tile([P, T], I32, name="tab", tag="tab_%d" % a, align_bytes=64)
+            tab = keep.tile([P, T], I32, name="tab", tag="wide_%d" % a, align_bytes=ALIGN)
             nc.sync.dma_start(out=tab[:], in_=tab_words[a].rearrange("p t i -> p (t i)").bitcast(I32))
             tabs.append(tab)
 
@@ -117,34 +125,38 @@ def tile_list_snow_cell_page_kernel(
         pages = {}
 
         def load_expo(i):
-            expos[i] = ring.tile([P, S], F32, name="expo_t", tag="expo_t", bufs=4)
+            expos[i] = ring.tile([P, S], F32, name="expo_t", tag="expo", bufs=EXPO_BUFS)
             nc.sync.dma_start(out=expos[i][:], in_=rows_of(expo, i))
 
         def load_page(i):
-            pages[i] = ring.tile([P, T2], F32, name="page", bufs=7)
+            pages[i] = ring.tile([P, T2], F32, name="page", bufs=PAGE_BUFS)
             nc.sync.dma_start(out=pages[i][:], in_=rows_of(page0, i))
 
         def load_wgs(t0, t1):
-            for q in (0, 2, 1, 3):
-                nc.sync.dma_start(out=wgs_t[32 * q : 32 * q + 32, t0:t1, :], in_=wgs_rows[:, t0:t1, :])
+            for g in (0, 2, 1, 3):
+                nc.sync.dma_start(out=wgs_t[QUAD * g : QUAD * (g + 1), t0:t1, :], in_=wgs_rows[:, t0:t1, :])
 
         load_expo(0)
         load_wgs(0, 1)
         load_expo(1)
         load_page(0)
-        w1_rest = [
-            keep.tile([P, PACK, PASS], F32, name="w1_rest", tag=("tab_0", "x_planes")[a], align_bytes=64) for a in range(2)
+        w1_second = [
+            keep.tile([P, PACK, PASS], F32, name="w1_second", tag=tag, align_bytes=ALIGN) for tag in ("wide_0", "x_pairs")
         ]
-        w1_later = [load_w1(w1_rest[a][:], a, 1) for a in range(2)]
+        for a in range(2):
+            load_w1(w1_second[a], a, 1)
         load_wgs(1, 2)
         load_page(1)
         load_expo(2)
         load_wgs(2, PACK)
         load_expo(3)
+        b4_t = keep.tile([P, N // P], F32, name="b4_t")
+        with nc.allow_non_contiguous_dma(reason="one bias value a partition"):
+            nc.sync.dma_start(out=b4_t[:], in_=b4.rearrange("(c p) -> p c", p=P))
         load_scale_rows(w4_sc, w4_scales)
 
-        w2_codes = keep.tile([P, 2, 2 * H], U8, name="w2_codes", align_bytes=64)
-        w2_sc = keep.tile([P, 2, H], U8, name="w2_sc", align_bytes=64)
+        w2_codes = keep.tile([P, 2, 2 * H], U8, name="w2_codes", align_bytes=ALIGN)
+        w2_sc = keep.tile([P, 2, H], U8, name="w2_sc", align_bytes=ALIGN)
         nc.vector.tensor_copy(
             out=w2_codes[:].bitcast(U16).rearrange("p a (b t m) -> p (a b) t m", b=2, t=PACK),
             in_=w2_raw[:].bitcast(U16).rearrange("p a (b m t) -> p (a b) t m", b=2, t=PACK),
@@ -155,16 +167,16 @@ def tile_list_snow_cell_page_kernel(
         )
         v_sc = []
         for a in range(2):
-            plane = keep.tile([P, S], U8, name="v_sc%d" % a, align_bytes=64)
+            plane = keep.tile([P, S], U8, name="v_sc%d" % a, align_bytes=ALIGN)
             nc.vector.tensor_copy(plane[:], tab_sc[:, a, :].indirect(pick[:]))
             v_sc.append(plane)
-        quantise_w1(0, round_w1(0, w1_raws))
-        v_codes = keep.tile([P, 2, S], U32, name="v_codes", tag="grouped_v", align_bytes=64)
+        quantise_w1(0, round_w1(w1_first, "v"), "chain")
+        v_codes = keep.tile([P, 2, S], U32, name="v_codes", tag="v", align_bytes=ALIGN)
         nc.vector.tensor_copy(v_codes[:, 0, :], tabs[0][:].bitcast(U32).indirect(pick[:]))
-        for h in range(2):
-            nc.vector.tensor_copy(v_codes[:, 1, half(h)], tabs[1][:].bitcast(U32).indirect(list_half(pick, h)))
+        for hf in range(2):
+            nc.vector.tensor_copy(v_codes[:, 1, half(hf)], tabs[1][:].bitcast(U32).indirect(list_half(pick, hf)))
 
-        def first_products(i, h):
+        def first_products(i, hf):
             b, t = divmod(i, PACK)
             wind = psum.tile([P, BANK], F32, name="wind", tag="acc")
             base = psum.tile([P, BANK], F32, name="base", tag="acc")
@@ -174,8 +186,8 @@ def tile_list_snow_cell_page_kernel(
                     out=wind[:],
                     lhsT=w2_codes[:, a, 2 * c2 : 2 * (c2 + P)].bitcast(FP4X4),
                     lhsT_scale=w2_sc[:, a, c2 : c2 + P],
-                    rhs=v_codes[:, a, half(h)].bitcast(FP8X4),
-                    rhs_scale=v_sc[a][:, half(h)],
+                    rhs=v_codes[:, a, half(hf)].bitcast(FP8X4),
+                    rhs_scale=v_sc[a][:, half(hf)],
                     start=(a == 0),
                     stop=(a == 1),
                 )
@@ -184,181 +196,182 @@ def tile_list_snow_cell_page_kernel(
                     out=base[:],
                     lhsT=w1_codes[b][:, c1 : c1 + P].bitcast(FP8X4),
                     lhsT_scale=w1_sc[:, b, c1 : c1 + P],
-                    rhs=v_codes[:, a, half(h)].bitcast(FP8X4),
-                    rhs_scale=v_sc[a][:, half(h)],
+                    rhs=v_codes[:, a, half(hf)].bitcast(FP8X4),
+                    rhs_scale=v_sc[a][:, half(hf)],
                     start=(a == 0),
                     stop=(a == 1),
                 )
             return base, wind
 
-        hs = {}
+        weighted = {}
 
         def make_h(i):
-            t = i % PACK
-            hw = keep.tile([P, S], F32, name="hw", tag="slot_%d" % i, align_bytes=64)
-            hs[i] = hw
-            if PATH[i] == "G":
-                base_sb = ring.tile([P, S], F32, name="base_sb", tag="base_sb", bufs=3)
-                banks = [first_products(i, h) for h in range(2)]
-                for h in range(2):
-                    nc.scalar.copy(out=hw[:, half(h)], in_=banks[h][1][:])
-                for h in range(2):
-                    nc.scalar.copy(out=base_sb[:, half(h)], in_=banks[h][0][:])
+            hw = keep.tile([P, S], F32, name="hw", tag=h_slot(i), align_bytes=ALIGN)
+            weighted[i] = hw
+            if i == 0:
+                sums = [first_products(i, hf) for hf in range(2)]
+                for hf, (base, wind) in enumerate(sums):
+                    nc.vector.tensor_tensor(hw[:, half(hf)], wind[:], expos[i][:, half(hf)], MULT)
+                for hf, (base, wind) in enumerate(sums):
+                    nc.vector.tensor_tensor(hw[:, half(hf)], base[:], hw[:, half(hf)], ADD)
+                nc.vector.tensor_tensor(hw[:], hw[:], wgs_t[:, i % PACK, :], MULT)
+            else:
+                base_sb = ring.tile([P, S], F32, name="base_sb", tag="base", bufs=H_AHEAD)
+                sums = [first_products(i, hf) for hf in range(2)]
+                for hf, (base, wind) in enumerate(sums):
+                    nc.scalar.copy(out=hw[:, half(hf)], in_=wind[:])
+                for hf, (base, wind) in enumerate(sums):
+                    nc.scalar.copy(out=base_sb[:, half(hf)], in_=base[:])
                 nc.gpsimd.tensor_tensor(hw[:], hw[:], expos[i][:], MULT)
                 nc.gpsimd.tensor_tensor(hw[:], hw[:], base_sb[:], ADD)
-                nc.gpsimd.tensor_tensor(hw[:], hw[:], wgs_t[:, t, :], MULT)
-            elif PATH[i] == "M":
-                base_sb = ring.tile([P, S], F32, name="base_sb", tag="base_sb", bufs=3)
-                for h in range(2):
-                    base, wind = first_products(i, h)
-                    nc.vector.tensor_tensor(hw[:, half(h)], wind[:], expos[i][:, half(h)], MULT)
-                    nc.scalar.copy(out=base_sb[:, half(h)], in_=base[:])
-                nc.gpsimd.tensor_tensor(hw[:], hw[:], base_sb[:], ADD)
-                nc.gpsimd.tensor_tensor(hw[:], hw[:], wgs_t[:, t, :], MULT)
-            else:
-                banks = [first_products(i, h) for h in range(2)]
-                for h in range(2):
-                    nc.vector.tensor_tensor(hw[:, half(h)], banks[h][1][:], expos[i][:, half(h)], MULT)
-                for h in range(2):
-                    nc.vector.tensor_tensor(hw[:, half(h)], banks[h][0][:], hw[:, half(h)], ADD)
-                if PATH[i] == "H":
-                    nc.vector.tensor_tensor(hw[:], hw[:], wgs_t[:, t, :], MULT)
+                nc.gpsimd.tensor_tensor(hw[:], hw[:], wgs_t[:, i % PACK, :], MULT)
 
         def scatter(i):
-            if PATH[i] in "GMH":
-                nc.vector.tensor_copy(pages[i][:].indirect(put[:]), hs[i][:])
-            elif PATH[i] == "V":
-                nc.vector.tensor_tensor(pages[i][:].indirect(put[:]), hs[i][:], wgs_t[:, i % PACK, :], MULT)
+            nc.vector.tensor_copy(pages[i][:].indirect(put[:]), weighted[i][:])
 
-        page_planes = {}
-        x_planes = {}
+        page_pairs = {}
+        x_pairs = {}
 
-        def after_scatter(i, last_inter):
-            b, t = divmod(i, PACK)
-            if t == 0:
-                page_planes[b] = keep.tile([P, PACK, T2], BF16, name="page_planes", tag="tab_%d" % b, align_bytes=64)
-                x_planes[b] = keep.tile([P, PACK, M], BF16, name="x_planes", tag="x_planes", align_bytes=64)
-            nc.sync.dma_start(out=rows_of(out_1, i), in_=pages[i][:])
-            xg = ring.tile([P, M], F32, name="xg", tag="xg", align_bytes=64)
-            if i < TILES - 1:
-                nc.vector.tensor_copy(xg[:], pages[i][:].indirect(read[:]))
-                nc.scalar.activation(out=x_planes[b][:, t, :], in_=xg[:], func=COPY, scale=sv_t[:, b, t : t + 1])
-                nc.scalar.copy(out=page_planes[b][:, t, :], in_=pages[i][:])
-            else:
-                for h in range(2):
-                    nc.vector.tensor_copy(xg[:, half(h)], pages[i][:].indirect(list_half(read, h)))
-                    nc.scalar.activation(
-                        out=last_inter[:].rearrange("p (m t) -> p m t", t=PACK)[:, half(h), t],
-                        in_=xg[:, half(h)],
-                        func=COPY,
-                        scale=sv_t[:, b, t : t + 1],
-                    )
-                    cols = slice(h * T2 // 2, (h + 1) * T2 // 2)
-                    nc.scalar.copy(out=page_planes[b][:, t, cols], in_=pages[i][:, cols])
+        def pair_place(pairs, t):
+            return pairs.rearrange("p (u m e) -> p u m e", u=2, e=2)[:, t // 2, :, t % 2]
 
-
-        def interleave(copy, dst, src):
+        def weave(copy, woven, pairs):
             copy(
-                out=dst.rearrange("p (c i t) -> p c t i", i=4, t=PACK),
-                in_=src.rearrange("p t (c i) -> p c t i", i=4),
+                out=woven.bitcast(F32).rearrange("p (c i u) -> p c u i", i=4, u=2),
+                in_=pairs.bitcast(F32).rearrange("p (u c i) -> p c u i", i=4, u=2),
             )
 
+        def page_half(b, hf):
+            return page_pairs[b][:, hf * PACK * T2 // 2 : (hf + 1) * PACK * T2 // 2]
+
+        def x_half(tile, hf):
+            return tile[:, hf * PACK * BANK : (hf + 1) * PACK * BANK]
+
+        def round_page(i, hf):
+            b, t = divmod(i, PACK)
+            nc.scalar.copy(out=pair_place(page_half(b, hf), t), in_=pages[i][:, hf * T2 // 2 : (hf + 1) * T2 // 2])
+
+        def scale_x(i, picked, hf):
+            b, t = divmod(i, PACK)
+            nc.scalar.activation(
+                out=pair_place(x_half(x_pairs[b], hf), t),
+                in_=picked[:, half(hf)],
+                func=COPY,
+                scale=sv_t[:, b, t : t + 1],
+            )
+
+        def after_scatter(i):
+            b, t = divmod(i, PACK)
+            if t == 0:
+                page_pairs[b] = keep.tile([P, PACK * T2], BF16, name="page_pairs", tag="wide_%d" % b, align_bytes=ALIGN)
+                x_pairs[b] = keep.tile([P, PACK * M], BF16, name="x_pairs", tag="x_pairs", align_bytes=ALIGN)
+            nc.sync.dma_start(out=rows_of(out_1, i), in_=pages[i][:])
+            picked = ring.tile([P, M], F32, name="picked", tag="picked", align_bytes=ALIGN)
+            if i < LAST:
+                for hf in range(2):
+                    round_page(i, hf)
+                nc.vector.tensor_copy(picked[:], pages[i][:].indirect(read[:]))
+                for hf in range(2):
+                    scale_x(i, picked, hf)
+            else:
+                round_page(i, 0)
+                for hf in range(2):
+                    nc.vector.tensor_copy(picked[:, half(hf)], pages[i][:].indirect(list_half(read, hf)))
+                    scale_x(i, picked, hf)
+                round_page(i, 1)
+
+        def weave_page(b, hf, copy):
+            woven = ring.tile([P, PACK * T2 // 2], BF16, name="page_woven", tag="stage", align_bytes=ALIGN)
+            weave(copy, woven[:], page_half(b, hf))
+            return woven
+
         x_codes = {}
-        x_sc = keep.tile([P, 2, M], U8, name="x_sc", align_bytes=64)
+        x_sc = {}
+        page_sc = {}
 
-        def weave_x(b, copy, h, inter):
-            interleave(copy, inter[:, h * BANK * PACK : (h + 1) * BANK * PACK], x_planes[b][:, :, half(h)])
-
-        def weave_page(b, c, copies):
-            inter = ring.tile([P, M * PACK], BF16, name="page_inter", tag="raw_inter", align_bytes=64)
-            for h in range(2):
-                c0 = c * 2 * BANK + h * BANK
-                interleave(copies[h], inter[:, h * BANK * PACK : (h + 1) * BANK * PACK], page_planes[b][:, :, c0 : c0 + BANK])
-            return inter
-
-        page_sc = [keep.tile([P, T2], U8, name="page_sc%d" % b, align_bytes=64) for b in range(2)]
-
-        def store_planes(b, c, inter, tag):
+        def store_planes(b, hf, woven, tag):
+            if hf == 0:
+                sc_tag = h_slot(LAST) if b == 0 else "page_sc"
+                page_sc[b] = keep.tile([P, T2], U8, name="page_sc", tag=sc_tag, align_bytes=ALIGN)
             words = out_2[b].rearrange("p m t -> p (m t)").bitcast(I32)
-            cols = slice(c * 2 * BANK, (c + 1) * 2 * BANK)
-            codes = keep.tile([P, 2 * BANK], U32, name="page_codes", tag=tag, align_bytes=64)
-            nc.vector.quantize_mx(out=codes[:].bitcast(FP8X4), scales=page_sc[b][:, cols], in_=inter[:])
-            nc.sync.dma_start(out=words[:, cols], in_=codes[:].bitcast(I32))
-            if c == 1:
-                for q in range(4):
-                    nc.sync.dma_start(
-                        out=out_3[b].rearrange("(g r) c -> r g c", r=4)[q].bitcast(I32),
-                        in_=page_sc[b][q:P:32, :].bitcast(I32),
+            codes = keep.tile([P, T2 // 2], U32, name="page_codes", tag=tag, align_bytes=ALIGN)
+            width = T2 // 4 if (b, hf) == (1, 1) else T2 // 2
+            for c0 in range(0, T2 // 2, width):
+                part = slice(c0, c0 + width)
+                cols = slice(hf * T2 // 2 + c0, hf * T2 // 2 + c0 + width)
+                nc.vector.quantize_mx(
+                    out=codes[:, part].bitcast(FP8X4),
+                    scales=page_sc[b][:, cols],
+                    in_=woven[:, c0 * PACK : (c0 + width) * PACK],
+                )
+                nc.sync.dma_start(out=words[:, cols], in_=codes[:, part].bitcast(I32))
+            if hf == 1:
+                queue = nc.sync if b == 0 else nc.scalar
+                for s in range(4):
+                    queue.dma_start(
+                        out=out_3[b].rearrange("(g row) c -> row g c", row=4)[s].bitcast(I32),
+                        in_=page_sc[b][s:P:QUAD, :].bitcast(I32),
                     )
 
-        w3_sc = keep.tile([P, 2 * N], U8, name="w3_sc", align_bytes=64)
-        w4_codes = keep.tile([P, 2, 2 * N], U8, name="w4_codes", align_bytes=64)
+        w4_codes = keep.tile([P, 2, 2 * N], U8, name="w4_codes", align_bytes=ALIGN)
 
         def round_w3():
-            grouped = keep.tile([P, 2 * N * PACK], BF16, name="w3_grouped", tag="tabsc_grouped", align_bytes=64)
+            rounded = keep.tile([P, 2 * N * PACK], BF16, name="w3_rounded", tag="chain", align_bytes=ALIGN)
             for a in range(2):
-                raw = ring.tile([P, PACK, N], F32, name="w3_raw", tag="raw_inter", align_bytes=64)
-                nc.sync.dma_start(out=raw[:], in_=w3[a * PASS : (a + 1) * PASS, :].rearrange("(p j) c -> p j c", j=PACK))
-                interleave(nc.scalar.copy, grouped[:, a * N * PACK : (a + 1) * N * PACK], raw[:])
+                raw = ring.tile([P, PACK, N], F32, name="w3_raw", tag="stage", align_bytes=ALIGN)
+                nc.sync.dma_start(out=raw[:], in_=w3[a * PASS : (a + 1) * PASS, :].rearrange("(p j) n -> p j n", j=PACK))
+                nc.scalar.copy(
+                    out=rounded[:, a * N * PACK : (a + 1) * N * PACK].rearrange("p (c i j) -> p c j i", i=4, j=PACK),
+                    in_=raw[:].rearrange("p j (c i) -> p c j i", i=4),
+                )
             nc.sync.dma_start(out=w4_codes[:].bitcast(I32), in_=w4_words.rearrange("a p c -> p a c").bitcast(I32))
-            return grouped
+            return rounded
 
-        on_scalar = [nc.scalar.copy] * 2
-        last_inter = None
-        make_h(0)
-        make_h(1)
-        make_h(2)
+        for i in range(H_AHEAD):
+            make_h(i)
         for i in range(TILES):
-            if i + 4 < TILES:
-                load_expo(i + 4)
+            if i + EXPO_BUFS < TILES:
+                load_expo(i + EXPO_BUFS)
             scatter(i)
             if i == 0:
-                w1_grouped = round_w1(1, w1_later)
+                w1_rounded = round_w1(w1_second, "chain")
             if i == 1:
-                quantise_w1(1, w1_grouped)
-                w3_grouped = round_w3()
-            if i == 4:
-                w3_codes = keep.tile([P, 2 * N], U32, name="w3_codes", tag="slot_4", align_bytes=64)
+                quantise_w1(1, w1_rounded, h_slot(1))
+                w3_rounded = round_w3()
+            if i == LAST - 1:
+                late_sc = keep.tile([P, M + 2 * N], U8, name="late_sc", tag=h_slot(i), align_bytes=ALIGN)
+                x_sc[0] = late_sc[:, :M]
+                w3_sc = late_sc[:, M:]
+                x_codes[0] = keep.tile([P, M], U32, name="x_codes", tag=h_slot(5), align_bytes=ALIGN)
+                nc.vector.quantize_mx(out=x_codes[0][:].bitcast(FP8X4), scales=x_sc[0], in_=x_woven[:])
+                w3_codes = keep.tile([P, 2 * N], U32, name="w3_codes", tag=h_slot(4), align_bytes=ALIGN)
                 for c0, c1 in ((0, 512), (512, 2 * N)):
                     nc.vector.quantize_mx(
                         out=w3_codes[:, c0:c1].bitcast(FP8X4),
                         scales=w3_sc[:, c0:c1],
-                        in_=w3_grouped[:, c0 * PACK : c1 * PACK],
+                        in_=w3_rounded[:, c0 * PACK : c1 * PACK],
                     )
-            if i == 5:
-                x_codes[0] = keep.tile([P, M], U32, name="x_codes", tag="slot_5", align_bytes=64)
-                nc.vector.quantize_mx(out=x_codes[0][:].bitcast(FP8X4), scales=x_sc[:, 0, :], in_=x_inter[:])
-                page_inter_1 = weave_page(0, 1, on_scalar)
-            if i == 6:
-                store_planes(0, 0, page_inter_0, "slot_6")
-            if i + 3 < TILES:
-                make_h(i + 3)
-            if i + 2 < TILES:
-                load_page(i + 2)
-            after_scatter(i, last_inter)
-            if i == TILES - 2:
-                last_inter = ring.tile([P, M * PACK], BF16, name="last_inter", tag="raw_inter", align_bytes=64)
-                for h in range(2):
-                    nc.scalar.copy(
-                        out=last_inter[:, h * BANK * PACK : (h + 1) * BANK * PACK].rearrange(
-                            "p (c i t) -> p c t i", i=4, t=PACK
-                        )[:, :, 0 : PACK - 1, :],
-                        in_=x_planes[1][:, 0 : PACK - 1, half(h)].rearrange("p t (c i) -> p c t i", i=4),
-                    )
+            if i + H_AHEAD < TILES:
+                make_h(i + H_AHEAD)
+            if i + PAGE_AHEAD < TILES:
+                load_page(i + PAGE_AHEAD)
+            after_scatter(i)
             if i == PACK - 1:
-                x_inter = ring.tile([P, M * PACK], BF16, name="x_inter", tag="raw_inter", align_bytes=64)
-                for h in range(2):
-                    weave_x(0, nc.scalar.copy, h, x_inter)
+                x_woven = ring.tile([P, M * PACK], BF16, name="x_woven", tag="stage", align_bytes=ALIGN)
+                for hf in range(2):
+                    weave(nc.scalar.copy, x_half(x_woven, hf), x_half(x_pairs[0], hf))
             if i == PACK:
-                page_inter_0 = weave_page(0, 0, on_scalar)
+                first_woven = weave_page(0, 0, nc.scalar.copy)
+            if i == LAST - 1:
+                second_woven = weave_page(0, 1, nc.scalar.copy)
 
-        def second_pass(bent, lin, a, c, h):
+        def last_products(bent, lin, a, c, hf):
             nc.tensor.matmul_mx(
                 out=bent[:],
                 lhsT=w4_codes[:, a, 2 * c * P : 2 * (c + 1) * P].bitcast(FP4X4),
                 lhsT_scale=w4_sc[:, a, c * P : (c + 1) * P],
-                rhs=x_codes[a][:, half(h)].bitcast(FP8X4),
-                rhs_scale=x_sc[:, a, half(h)],
+                rhs=x_codes[a][:, half(hf)].bitcast(FP8X4),
+                rhs_scale=x_sc[a][:, half(hf)],
                 start=(a == 0),
                 stop=(a == 1),
             )
@@ -367,41 +380,43 @@ def tile_list_snow_cell_page_kernel(
                 out=lin[:],
                 lhsT=w3_codes[:, c3 : c3 + P].bitcast(FP8X4),
                 lhsT_scale=w3_sc[:, c3 : c3 + P],
-                rhs=x_codes[a][:, half(h)].bitcast(FP8X4),
-                rhs_scale=x_sc[:, a, half(h)],
+                rhs=x_codes[a][:, half(hf)].bitcast(FP8X4),
+                rhs_scale=x_sc[a][:, half(hf)],
                 start=(a == 0),
                 stop=(a == 1),
             )
 
-        blocks = [(h, c) for h in range(2) for c in range(N // P)]
-        sums = {}
+        blocks = [(hf, c) for hf in range(2) for c in range(N // P)]
+        open_sums = {}
 
-        def open_block(h, c):
+        def open_block(hf, c):
             bent = psum.tile([P, BANK], F32, name="bent", tag="acc")
             lin = psum.tile([P, BANK], F32, name="lin", tag="acc")
-            sums[h, c] = (bent, lin)
-            second_pass(bent, lin, 0, c, h)
+            open_sums[hf, c] = (bent, lin)
+            last_products(bent, lin, 0, c, hf)
 
-        for h, c in blocks[:4]:
-            open_block(h, c)
-        x_codes[1] = keep.tile([P, M], U32, name="x_codes", tag="slot_0", align_bytes=64)
-        for h in range(2):
+        for hf, c in blocks[:OPEN_BLOCKS]:
+            open_block(hf, c)
+        x_sc[1] = keep.tile([P, M], U8, name="x_sc", align_bytes=ALIGN)
+        x_codes[1] = keep.tile([P, M], U32, name="x_codes", tag=h_slot(0), align_bytes=ALIGN)
+        last_woven = keep.tile([P, M * PACK], BF16, name="last_woven", tag="chain", align_bytes=ALIGN)
+        for hf in range(2):
+            weave(nc.vector.tensor_copy, x_half(last_woven, hf), x_half(x_pairs[1], hf))
             nc.vector.quantize_mx(
-                out=x_codes[1][:, half(h)].bitcast(FP8X4),
-                scales=x_sc[:, 1, half(h)],
-                in_=last_inter[:, h * BANK * PACK : (h + 1) * BANK * PACK],
+                out=x_codes[1][:, half(hf)].bitcast(FP8X4), scales=x_sc[1][:, half(hf)], in_=x_half(last_woven, hf)
             )
-        store_planes(0, 1, page_inter_1, "slot_7")
-        store_planes(1, 0, weave_page(1, 0, [nc.vector.tensor_copy, nc.vector.tensor_copy]), "slot_2")
-        for n, (h, c) in enumerate(blocks):
-            bent, lin = sums[h, c]
-            second_pass(bent, lin, 1, c, h)
-            curve = ring.tile([P, BANK], F32, name="curve", tag="base_sb", bufs=3)
+        store_planes(0, 0, first_woven, h_slot(2))
+        store_planes(0, 1, second_woven, h_slot(3))
+        store_planes(1, 0, weave_page(1, 0, nc.scalar.copy), "planes_0")
+        for n, (hf, c) in enumerate(blocks):
+            bent, lin = open_sums[hf, c]
+            last_products(bent, lin, 1, c, hf)
+            curve = ring.tile([P, BANK], F32, name="curve", tag="base", bufs=H_AHEAD)
             nc.scalar.activation(out=curve[:], in_=bent[:], func=TANH, bias=b4_t[:, c : c + 1])
-            y = ring.tile([P, BANK], F32, name="y", tag="expo_t", bufs=4)
+            y = ring.tile([P, BANK], F32, name="y", tag="expo", bufs=EXPO_BUFS)
             nc.vector.tensor_tensor(y[:], lin[:], curve[:], ADD)
-            nc.sync.dma_start(out=out_0[c * P : (c + 1) * P, half(h)], in_=y[:])
-            if n + 4 < len(blocks):
-                open_block(*blocks[n + 4])
-            if n == 2:
-                store_planes(1, 1, weave_page(1, 1, [nc.vector.tensor_copy, nc.scalar.copy]), "slot_3")
+            nc.sync.dma_start(out=out_0[c * P : (c + 1) * P, half(hf)], in_=y[:])
+            if n + OPEN_BLOCKS < len(blocks):
+                open_block(*blocks[n + OPEN_BLOCKS])
+            if (hf, c) == (0, N // P - 1):
+                store_planes(1, 1, weave_page(1, 1, nc.vector.tensor_copy), "planes_1")

from contextlib import ExitStack

import concourse.mybir as mybir

K, H, N, T, S, T2, M = 1024, 1024, 384, 4096, 1024, 2048, 1024
FLOPS = 2 * 2 * K * H * S + 2 * 2 * H * N * M

F32 = mybir.dt.float32
BF16 = mybir.dt.bfloat16
I32 = mybir.dt.int32
U32 = mybir.dt.uint32
U16 = mybir.dt.uint16
U8 = mybir.dt.uint8
FP8X4 = mybir.dt.float8_e4m3fn_x4
FP4X4 = mybir.dt.float4_e2m1fn_x4
MULT = mybir.AluOpType.mult
ADD = mybir.AluOpType.add
COPY = mybir.ActivationFunctionType.Copy
TANH = mybir.ActivationFunctionType.Tanh

P = 128
QUAD = 32
PACK = 4
PASS = P * PACK
BANK = 512
TILES = H // P
LAST = TILES - 1
ALIGN = 64
H_AHEAD = 3
EXPO_BUFS = H_AHEAD + 1
PAGE_AHEAD = 2
PAGE_BUFS = 6
OPEN_BLOCKS = 4


def tile_list_snow_cell_page_kernel(
    tc, tab_words, tab_scales, offs, offs2, offs3, w1, w2_words, w2_scales, expo, page0, wgs, sv,
    w3, w4_words, w4_scales, b4, out_0, out_1, out_2, out_3,
):
    nc = tc.nc
    with ExitStack() as ctx:
        lists = ctx.enter_context(tc.tile_pool(name="lists", bufs=1))
        keep = ctx.enter_context(tc.tile_pool(name="keep", bufs=1))
        ring = ctx.enter_context(tc.tile_pool(name="ring", bufs=2))
        psum = ctx.enter_context(tc.psum_pool(name="psum", bufs=8))

        def rows_of(mat, i):
            b, t = divmod(i, PACK)
            return mat[b * PASS : (b + 1) * PASS, :].rearrange("(p t) c -> p t c", t=PACK)[:, t, :]

        def half(hf):
            return slice(hf * BANK, (hf + 1) * BANK)

        def list_half(lst, hf):
            return lst[:, hf * (BANK // 16) : (hf + 1) * (BANK // 16)]

        def h_slot(i):
            return "h_slot_%d" % i

        pick = lists.tile([P, S // 16], U16, name="pick")
        put = lists.tile([P, S // 16], U16, name="put")
        read = lists.tile([P, M // 16], U16, name="read")
        nc.sync.dma_start(pick[:], offs)
        nc.sync.dma_start(put[:], offs2)
        nc.sync.dma_start(read[:], offs3)

        def load_scale_rows(planes, src):
            for s in range(4):
                nc.sync.dma_start(
                    out=planes[s:P:QUAD, :, :].bitcast(I32),
                    in_=src.rearrange("a (g row) c -> row g a c", row=4)[s].bitcast(I32),
                )

        tab_sc = keep.tile([P, 2, T], U8, name="tab_sc", tag="chain", align_bytes=ALIGN)
        w2_sc_raw = keep.tile([P, 2, H], U8, name="w2_sc_raw", align_bytes=ALIGN)
        w4_sc = keep.tile([P, 2, N], U8, name="w4_sc", align_bytes=ALIGN)
        for planes in (w2_sc_raw, tab_sc, w4_sc):
            nc.vector.memset(planes[:].bitcast(I32), 0)

        w2_raw = ring.tile([P, 2, 2 * H], U8, name="w2_raw", tag="picked", align_bytes=ALIGN)
        for a in range(2):
            for b in range(2):
                cols = slice(b * 2 * PASS, (b + 1) * 2 * PASS)
                nc.sync.dma_start(out=w2_raw[:, a, cols].bitcast(I32), in_=w2_words[a][:, cols].bitcast(I32))

        w1_codes = {}
        w1_sc = keep.tile([P, 2, 2 * PASS], U8, name="w1_sc", align_bytes=ALIGN)

        def load_w1(raw, a, b):
            src = w1[a * PASS : (a + 1) * PASS, b * PASS : (b + 1) * PASS]
            nc.sync.dma_start(out=raw[:], in_=src.rearrange("(p j) c -> p j c", j=PACK))

        def round_w1(raws, tag):
            rounded = keep.tile([P, 2 * PASS * PACK], BF16, name="w1_rounded", tag=tag, align_bytes=ALIGN)
            for a in range(2):
                nc.scalar.copy(
                    out=rounded[:, a * PASS * PACK : (a + 1) * PASS * PACK].rearrange(
                        "p (t m j) -> p m t j", t=PACK, j=PACK
                    ),
                    in_=raws[a][:].rearrange("p j (m t) -> p m t j", t=PACK),
                )
            return rounded

        def quantise_w1(b, rounded, tag):
            w1_codes[b] = keep.tile([P, 2 * PASS], U32, name="w1_codes", tag=tag, align_bytes=ALIGN)
            nc.vector.quantize_mx(out=w1_codes[b][:].bitcast(FP8X4), scales=w1_sc[:, b, :], in_=rounded[:])

        w1_first = [ring.tile([P, PACK, PASS], F32, name="w1_first", tag="stage", align_bytes=ALIGN) for a in range(2)]
        sv_t = keep.tile([P, 2, PACK], F32, name="sv_t")
        nc.sync.dma_start(out=sv_t[:], in_=sv.rearrange("(b p t) -> p b t", b=2, t=PACK))
        load_scale_rows(w2_sc_raw, w2_scales)
        load_scale_rows(tab_sc, tab_scales)
        for a in range(2):
            load_w1(w1_first[a], a, 0)

        tabs = []
        for a in range(2):
            tab = keep.tile([P, T], I32, name="tab", tag="wide_%d" % a, align_bytes=ALIGN)
            nc.sync.dma_start(out=tab[:], in_=tab_words[a].rearrange("p t i -> p (t i)").bitcast(I32))
            tabs.append(tab)

        wgs_t = keep.tile([P, PACK, S], F32, name="wgs_t")
        wgs_rows = wgs.rearrange("(q t) j -> q t j", t=PACK)
        expos = {}
        pages = {}

        def load_expo(i):
            expos[i] = ring.tile([P, S], F32, name="expo_t", tag="expo", bufs=EXPO_BUFS)
            nc.sync.dma_start(out=expos[i][:], in_=rows_of(expo, i))

        def load_page(i):
            pages[i] = ring.tile([P, T2], F32, name="page", bufs=PAGE_BUFS)
            nc.sync.dma_start(out=pages[i][:], in_=rows_of(page0, i))

        def load_wgs(t0, t1):
            for g in (0, 2, 1, 3):
                nc.sync.dma_start(out=wgs_t[QUAD * g : QUAD * (g + 1), t0:t1, :], in_=wgs_rows[:, t0:t1, :])

        load_expo(0)
        load_wgs(0, 1)
        load_expo(1)
        load_page(0)
        w1_second = [
            keep.tile([P, PACK, PASS], F32, name="w1_second", tag=tag, align_bytes=ALIGN) for tag in ("wide_0", "x_pairs")
        ]
        for a in range(2):
            load_w1(w1_second[a], a, 1)
        load_wgs(1, 2)
        load_page(1)
        load_expo(2)
        load_wgs(2, PACK)
        load_expo(3)
        b4_t = keep.tile([P, N // P], F32, name="b4_t")
        with nc.allow_non_contiguous_dma(reason="one bias value a partition"):
            nc.sync.dma_start(out=b4_t[:], in_=b4.rearrange("(c p) -> p c", p=P))
        load_scale_rows(w4_sc, w4_scales)

        w2_codes = keep.tile([P, 2, 2 * H], U8, name="w2_codes", align_bytes=ALIGN)
        w2_sc = keep.tile([P, 2, H], U8, name="w2_sc", align_bytes=ALIGN)
        nc.vector.tensor_copy(
            out=w2_codes[:].bitcast(U16).rearrange("p a (b t m) -> p (a b) t m", b=2, t=PACK),
            in_=w2_raw[:].bitcast(U16).rearrange("p a (b m t) -> p (a b) t m", b=2, t=PACK),
        )
        nc.vector.tensor_copy(
            out=w2_sc[:].rearrange("p a (b t m) -> p (a b) t m", b=2, t=PACK),
            in_=w2_sc_raw[:].rearrange("p a (b m t) -> p (a b) t m", b=2, t=PACK),
        )
        v_sc = []
        for a in range(2):
            plane = keep.tile([P, S], U8, name="v_sc%d" % a, align_bytes=ALIGN)
            nc.vector.tensor_copy(plane[:], tab_sc[:, a, :].indirect(pick[:]))
            v_sc.append(plane)
        quantise_w1(0, round_w1(w1_first, "v"), "chain")
        v_codes = keep.tile([P, 2, S], U32, name="v_codes", tag="v", align_bytes=ALIGN)
        nc.vector.tensor_copy(v_codes[:, 0, :], tabs[0][:].bitcast(U32).indirect(pick[:]))
        for hf in range(2):
            nc.vector.tensor_copy(v_codes[:, 1, half(hf)], tabs[1][:].bitcast(U32).indirect(list_half(pick, hf)))

        def first_products(i, hf):
            b, t = divmod(i, PACK)
            wind = psum.tile([P, BANK], F32, name="wind", tag="acc")
            base = psum.tile([P, BANK], F32, name="base", tag="acc")
            for a in range(2):
                c2 = b * PASS + t * P
                nc.tensor.matmul_mx(
                    out=wind[:],
                    lhsT=w2_codes[:, a, 2 * c2 : 2 * (c2 + P)].bitcast(FP4X4),
                    lhsT_scale=w2_sc[:, a, c2 : c2 + P],
                    rhs=v_codes[:, a, half(hf)].bitcast(FP8X4),
                    rhs_scale=v_sc[a][:, half(hf)],
                    start=(a == 0),
                    stop=(a == 1),
                )
                c1 = a * PASS + t * P
                nc.tensor.matmul_mx(
                    out=base[:],
                    lhsT=w1_codes[b][:, c1 : c1 + P].bitcast(FP8X4),
                    lhsT_scale=w1_sc[:, b, c1 : c1 + P],
                    rhs=v_codes[:, a, half(hf)].bitcast(FP8X4),
                    rhs_scale=v_sc[a][:, half(hf)],
                    start=(a == 0),
                    stop=(a == 1),
                )
            return base, wind

        weighted = {}

        def make_h(i):
            hw = keep.tile([P, S], F32, name="hw", tag=h_slot(i), align_bytes=ALIGN)
            weighted[i] = hw
            if i == 0:
                sums = [first_products(i, hf) for hf in range(2)]
                for hf, (base, wind) in enumerate(sums):
                    nc.vector.tensor_tensor(hw[:, half(hf)], wind[:], expos[i][:, half(hf)], MULT)
                for hf, (base, wind) in enumerate(sums):
                    nc.vector.tensor_tensor(hw[:, half(hf)], base[:], hw[:, half(hf)], ADD)
                nc.vector.tensor_tensor(hw[:], hw[:], wgs_t[:, i % PACK, :], MULT)
            else:
                base_sb = ring.tile([P, S], F32, name="base_sb", tag="base", bufs=H_AHEAD)
                sums = [first_products(i, hf) for hf in range(2)]
                for hf, (base, wind) in enumerate(sums):
                    nc.scalar.copy(out=hw[:, half(hf)], in_=wind[:])
                for hf, (base, wind) in enumerate(sums):
                    nc.scalar.copy(out=base_sb[:, half(hf)], in_=base[:])
                nc.gpsimd.tensor_tensor(hw[:], hw[:], expos[i][:], MULT)
                nc.gpsimd.tensor_tensor(hw[:], hw[:], base_sb[:], ADD)
                nc.gpsimd.tensor_tensor(hw[:], hw[:], wgs_t[:, i % PACK, :], MULT)

        def scatter(i):
            nc.vector.tensor_copy(pages[i][:].indirect(put[:]), weighted[i][:])

        page_pairs = {}
        x_pairs = {}

        def pair_place(pairs, t):
            return pairs.rearrange("p (u m e) -> p u m e", u=2, e=2)[:, t // 2, :, t % 2]

        def weave(copy, woven, pairs):
            copy(
                out=woven.bitcast(F32).rearrange("p (c i u) -> p c u i", i=4, u=2),
                in_=pairs.bitcast(F32).rearrange("p (u c i) -> p c u i", i=4, u=2),
            )

        def page_half(b, hf):
            return page_pairs[b][:, hf * PACK * T2 // 2 : (hf + 1) * PACK * T2 // 2]

        def x_half(tile, hf):
            return tile[:, hf * PACK * BANK : (hf + 1) * PACK * BANK]

        def round_page(i, hf):
            b, t = divmod(i, PACK)
            nc.scalar.copy(out=pair_place(page_half(b, hf), t), in_=pages[i][:, hf * T2 // 2 : (hf + 1) * T2 // 2])

        def scale_x(i, picked, hf):
            b, t = divmod(i, PACK)
            nc.scalar.activation(
                out=pair_place(x_half(x_pairs[b], hf), t),
                in_=picked[:, half(hf)],
                func=COPY,
                scale=sv_t[:, b, t : t + 1],
            )

        def after_scatter(i):
            b, t = divmod(i, PACK)
            if t == 0:
                page_pairs[b] = keep.tile([P, PACK * T2], BF16, name="page_pairs", tag="wide_%d" % b, align_bytes=ALIGN)
                x_pairs[b] = keep.tile([P, PACK * M], BF16, name="x_pairs", tag="x_pairs", align_bytes=ALIGN)
            nc.sync.dma_start(out=rows_of(out_1, i), in_=pages[i][:])
            picked = ring.tile([P, M], F32, name="picked", tag="picked", align_bytes=ALIGN)
            if i < LAST:
                for hf in range(2):
                    round_page(i, hf)
                nc.vector.tensor_copy(picked[:], pages[i][:].indirect(read[:]))
                for hf in range(2):
                    scale_x(i, picked, hf)
            else:
                round_page(i, 0)
                for hf in range(2):
                    nc.vector.tensor_copy(picked[:, half(hf)], pages[i][:].indirect(list_half(read, hf)))
                    scale_x(i, picked, hf)
                round_page(i, 1)

        def weave_page(b, hf, copy):
            woven = ring.tile([P, PACK * T2 // 2], BF16, name="page_woven", tag="stage", align_bytes=ALIGN)
            weave(copy, woven[:], page_half(b, hf))
            return woven

        x_codes = {}
        x_sc = {}
        page_sc = {}

        def store_planes(b, hf, woven, tag):
            if hf == 0:
                sc_tag = h_slot(LAST) if b == 0 else "page_sc"
                page_sc[b] = keep.tile([P, T2], U8, name="page_sc", tag=sc_tag, align_bytes=ALIGN)
            words = out_2[b].rearrange("p m t -> p (m t)").bitcast(I32)
            codes = keep.tile([P, T2 // 2], U32, name="page_codes", tag=tag, align_bytes=ALIGN)
            width = T2 // 4 if (b, hf) == (1, 1) else T2 // 2
            for c0 in range(0, T2 // 2, width):
                part = slice(c0, c0 + width)
                cols = slice(hf * T2 // 2 + c0, hf * T2 // 2 + c0 + width)
                nc.vector.quantize_mx(
                    out=codes[:, part].bitcast(FP8X4),
                    scales=page_sc[b][:, cols],
                    in_=woven[:, c0 * PACK : (c0 + width) * PACK],
                )
                nc.sync.dma_start(out=words[:, cols], in_=codes[:, part].bitcast(I32))
            if hf == 1:
                queue = nc.sync if b == 0 else nc.scalar
                for s in range(4):
                    queue.dma_start(
                        out=out_3[b].rearrange("(g row) c -> row g c", row=4)[s].bitcast(I32),
                        in_=page_sc[b][s:P:QUAD, :].bitcast(I32),
                    )

        w4_codes = keep.tile([P, 2, 2 * N], U8, name="w4_codes", align_bytes=ALIGN)

        def round_w3():
            rounded = keep.tile([P, 2 * N * PACK], BF16, name="w3_rounded", tag="chain", align_bytes=ALIGN)
            for a in range(2):
                raw = ring.tile([P, PACK, N], F32, name="w3_raw", tag="stage", align_bytes=ALIGN)
                nc.sync.dma_start(out=raw[:], in_=w3[a * PASS : (a + 1) * PASS, :].rearrange("(p j) n -> p j n", j=PACK))
                nc.scalar.copy(
                    out=rounded[:, a * N * PACK : (a + 1) * N * PACK].rearrange("p (c i j) -> p c j i", i=4, j=PACK),
                    in_=raw[:].rearrange("p j (c i) -> p c j i", i=4),
                )
            nc.sync.dma_start(out=w4_codes[:].bitcast(I32), in_=w4_words.rearrange("a p c -> p a c").bitcast(I32))
            return rounded

        for i in range(H_AHEAD):
            make_h(i)
        for i in range(TILES):
            if i + EXPO_BUFS < TILES:
                load_expo(i + EXPO_BUFS)
            scatter(i)
            if i == 0:
                w1_rounded = round_w1(w1_second, "chain")
            if i == 1:
                quantise_w1(1, w1_rounded, h_slot(1))
                w3_rounded = round_w3()
            if i == LAST - 1:
                late_sc = keep.tile([P, M + 2 * N], U8, name="late_sc", tag=h_slot(i), align_bytes=ALIGN)
                x_sc[0] = late_sc[:, :M]
                w3_sc = late_sc[:, M:]
                x_codes[0] = keep.tile([P, M], U32, name="x_codes", tag=h_slot(5), align_bytes=ALIGN)
                nc.vector.quantize_mx(out=x_codes[0][:].bitcast(FP8X4), scales=x_sc[0], in_=x_woven[:])
                w3_codes = keep.tile([P, 2 * N], U32, name="w3_codes", tag=h_slot(4), align_bytes=ALIGN)
                for c0, c1 in ((0, 512), (512, 2 * N)):
                    nc.vector.quantize_mx(
                        out=w3_codes[:, c0:c1].bitcast(FP8X4),
                        scales=w3_sc[:, c0:c1],
                        in_=w3_rounded[:, c0 * PACK : c1 * PACK],
                    )
            if i + H_AHEAD < TILES:
                make_h(i + H_AHEAD)
            if i + PAGE_AHEAD < TILES:
                load_page(i + PAGE_AHEAD)
            after_scatter(i)
            if i == PACK - 1:
                x_woven = ring.tile([P, M * PACK], BF16, name="x_woven", tag="stage", align_bytes=ALIGN)
                for hf in range(2):
                    weave(nc.scalar.copy, x_half(x_woven, hf), x_half(x_pairs[0], hf))
            if i == PACK:
                first_woven = weave_page(0, 0, nc.scalar.copy)
            if i == LAST - 1:
                second_woven = weave_page(0, 1, nc.scalar.copy)

        def last_products(bent, lin, a, c, hf):
            nc.tensor.matmul_mx(
                out=bent[:],
                lhsT=w4_codes[:, a, 2 * c * P : 2 * (c + 1) * P].bitcast(FP4X4),
                lhsT_scale=w4_sc[:, a, c * P : (c + 1) * P],
                rhs=x_codes[a][:, half(hf)].bitcast(FP8X4),
                rhs_scale=x_sc[a][:, half(hf)],
                start=(a == 0),
                stop=(a == 1),
            )
            c3 = a * N + c * P
            nc.tensor.matmul_mx(
                out=lin[:],
                lhsT=w3_codes[:, c3 : c3 + P].bitcast(FP8X4),
                lhsT_scale=w3_sc[:, c3 : c3 + P],
                rhs=x_codes[a][:, half(hf)].bitcast(FP8X4),
                rhs_scale=x_sc[a][:, half(hf)],
                start=(a == 0),
                stop=(a == 1),
            )

        blocks = [(hf, c) for hf in range(2) for c in range(N // P)]
        open_sums = {}

        def open_block(hf, c):
            bent = psum.tile([P, BANK], F32, name="bent", tag="acc")
            lin = psum.tile([P, BANK], F32, name="lin", tag="acc")
            open_sums[hf, c] = (bent, lin)
            last_products(bent, lin, 0, c, hf)

        for hf, c in blocks[:OPEN_BLOCKS]:
            open_block(hf, c)
        x_sc[1] = keep.tile([P, M], U8, name="x_sc", align_bytes=ALIGN)
        x_codes[1] = keep.tile([P, M], U32, name="x_codes", tag=h_slot(0), align_bytes=ALIGN)
        last_woven = keep.tile([P, M * PACK], BF16, name="last_woven", tag="chain", align_bytes=ALIGN)
        for hf in range(2):
            weave(nc.vector.tensor_copy, x_half(last_woven, hf), x_half(x_pairs[1], hf))
            nc.vector.quantize_mx(
                out=x_codes[1][:, half(hf)].bitcast(FP8X4), scales=x_sc[1][:, half(hf)], in_=x_half(last_woven, hf)
            )
        store_planes(0, 0, first_woven, h_slot(2))
        store_planes(0, 1, second_woven, h_slot(3))
        store_planes(1, 0, weave_page(1, 0, nc.scalar.copy), "planes_0")
        for n, (hf, c) in enumerate(blocks):
            bent, lin = open_sums[hf, c]
            last_products(bent, lin, 1, c, hf)
            curve = ring.tile([P, BANK], F32, name="curve", tag="base", bufs=H_AHEAD)
            nc.scalar.activation(out=curve[:], in_=bent[:], func=TANH, bias=b4_t[:, c : c + 1])
            y = ring.tile([P, BANK], F32, name="y", tag="expo", bufs=EXPO_BUFS)
            nc.vector.tensor_tensor(y[:], lin[:], curve[:], ADD)
            nc.sync.dma_start(out=out_0[c * P : (c + 1) * P, half(hf)], in_=y[:])
            if n + OPEN_BLOCKS < len(blocks):
                open_block(*blocks[n + OPEN_BLOCKS])
            if (hf, c) == (0, N // P - 1):
                store_planes(1, 1, weave_page(1, 1, nc.vector.tensor_copy), "planes_1")
